import numpy as np
import ml_dtypes


def mxq(x, axis, fmt="e4m3"):
    dtype, down = {"e4m3": (ml_dtypes.float8_e4m3fn, 7), "e5m2": (ml_dtypes.float8_e5m2, 14)}[fmt]
    v = np.moveaxis(np.asarray(x, np.float32).astype(ml_dtypes.bfloat16).astype(np.float64), axis, -1)
    blocks = v.reshape(v.shape[:-1] + (-1, 32))
    amax = np.abs(blocks).max(-1, keepdims=True)
    byte = np.maximum(np.where(amax > 0, np.frexp(amax)[1] - 1 + 127, 0) - down, 1)
    scale = np.exp2(byte - 127.0)
    codes = (blocks / scale).astype(np.float32).astype(dtype).astype(np.float64)
    return np.moveaxis((codes * scale).reshape(v.shape), -1, axis)


WIDE = False


def mx_kscale(k):
    if not WIDE:
        return np.ones(k)
    levels = np.array([10, -10, 5, -5, 0])
    if k % 512:
        return np.exp2(np.random.permutation(np.resize(levels, k // 32))).repeat(32)
    a = np.empty((k // 512, 16))
    for p in range(k // 512):
        a[p, :8] = np.random.permutation(np.resize(levels, 8))
        for g in range(8):
            far = levels[np.abs(levels - a[p, g]) >= 10]
            a[p, g + 8] = far[np.random.randint(len(far))]
    return np.exp2(a.ravel()).repeat(32)


def f64(x):
    return np.asarray(x).astype(np.float64)


def striped(idx):
    return np.tile(idx.reshape(-1, 16).T, (8, 1)).astype(np.uint16)


def unstriped(offs):
    return offs[:16].T.reshape(-1).astype(np.int64)


E2M1 = np.array([0.0, 0.5, 1.0, 1.5, 2.0, 3.0, 4.0, 6.0, -0.0, -0.5, -1.0, -1.5, -2.0, -3.0, -4.0, -6.0])


def pack_weight(w, fmt):
    k, n = w.shape
    w = f64(np.asarray(w, np.float32).astype(ml_dtypes.bfloat16)).reshape(k // 32, 32, n)
    amax = np.abs(w).max(1)
    if fmt == "e4m3":
        byte = np.frexp(amax)[1] - 1 + 127 - 7
    else:
        mant, ex = np.frexp(amax / 6.0)
        byte = np.where(mant > 0.5, ex, ex - 1) + 127
    byte = np.clip(np.where(amax > 0, byte, 1), 1, 254)
    scaled = (w * np.exp2(127.0 - byte)[:, None, :]).reshape(k, n).astype(np.float32)
    by_word = np.ascontiguousarray(scaled.reshape(k // 512, 128, 4, n).transpose(0, 1, 3, 2))
    if fmt == "e4m3":
        words = by_word.astype(ml_dtypes.float8_e4m3fn).view(np.uint8)
    else:
        c = by_word.astype(ml_dtypes.float4_e2m1fn).view(np.uint8) & 0xF
        words = (c[..., 0::2] | (c[..., 1::2] << 4)).reshape(k // 512, 128, 2 * n)
    return np.ascontiguousarray(words), np.ascontiguousarray(byte.astype(np.uint8).reshape(k // 512, 16, n))


def unpack_weight(words, scales, fmt):
    g, _, n = scales.shape
    words = np.ascontiguousarray(words).reshape(g, 128, n, -1)
    if fmt == "e4m3":
        vals = words.view(ml_dtypes.float8_e4m3fn).astype(np.float64)
    else:
        nib = np.empty((g, 128, n, 4), np.uint8)
        nib[..., 0::2] = words & 0xF
        nib[..., 1::2] = words >> 4
        vals = E2M1[nib]
    vals = vals * np.repeat(np.exp2(scales.astype(np.float64) - 127.0), 8, axis=1)[..., None]
    return vals.transpose(0, 1, 3, 2).reshape(g * 512, n)


K, T, E, C, N = 512, 512, 12, 128, 256
TOP = 3


def by_expert(wq, xq):
    return np.concatenate([wq[e].T @ xq[:, e * C:(e + 1) * C] for e in range(E)], axis=1)


def setup_inputs():
    n = np.random.standard_normal
    s = mx_kscale(K)[:, None]
    deal = np.repeat(np.arange(E), C).reshape(TOP, T)[:, np.random.permutation(T)]
    deal = np.take_along_axis(deal, np.argsort(np.random.rand(TOP, T), axis=0), axis=0)
    for _ in range(8):
        s_, t_ = np.random.permutation(T).reshape(2, -1); r = np.random.randint(TOP, size=T // 2); x, y = deal[r, s_].copy(), deal[r, t_].copy()
        ok = ~((deal[:, s_] == y).any(0) | (deal[:, t_] == x).any(0)); deal[r[ok], s_[ok]] = y[ok]; deal[r[ok], t_[ok]] = x[ok]
    order = np.lexsort((np.random.rand(TOP * T), deal.reshape(-1)))
    slot_token = order % T; pos = np.empty(TOP * T, np.int64); pos[order] = np.arange(TOP * T); pos = pos.reshape(TOP, T)
    g = np.random.uniform(0.5, 1.5, (TOP, T)); g = g / g.sum(0)
    w = [pack_weight(m, "e2m1") for m in n((E, K, N)) / np.sqrt(K) / s[None]]
    w_slot = np.empty(E * C)
    for r in range(TOP): w_slot[pos[r]] = g[r]
    return {
        "xT": (n((K, T)) * s).astype(np.float32),
        "w_words": np.stack([m[0] for m in w]),
        "w_scales": np.stack([m[1] for m in w]),
        "gate": np.tile(w_slot, (K, 1)).astype(np.float32),
        "offs": striped(slot_token),
        "pos1": striped(pos[0]),
        "pos2": striped(pos[1]),
        "pos3": striped(pos[2]),
    }


def reference(xT, w_words, w_scales, gate, offs, pos1, pos2, pos3):
    idx = unstriped(offs)
    w = np.stack([unpack_weight(w_words[e], w_scales[e], "e2m1") for e in range(E)])
    xq = mxq(f64(gate) * f64(xT)[:, idx], 0, "e4m3")
    y = by_expert(w, xq)
    return y[:, unstriped(pos1)] + y[:, unstriped(pos2)] + y[:, unstriped(pos3)]

@@ -1,0 +1,171 @@
+from contextlib import ExitStack
+
+import concourse.mybir as mybir
+
+K, T, E, C, N = 512, 512, 12, 128, 256
+S = E * C
+P = 128
+PACK = 4
+FLOPS = 2 * K * N * S
+BYTES = 4 * K * T + E * P * 2 * N + E * 16 * N + 4 * S + 2 * P * (S + 3 * T) // 16 + 4 * N * T
+
+F32 = mybir.dt.float32
+BF16 = mybir.dt.bfloat16
+I32 = mybir.dt.int32
+U32 = mybir.dt.uint32
+U16 = mybir.dt.uint16
+U8 = mybir.dt.uint8
+FP8X4 = mybir.dt.float8_e4m3fn_x4
+FP4X4 = mybir.dt.float4_e2m1fn_x4
+MULT = mybir.AluOpType.mult
+ADD = mybir.AluOpType.add
+
+PIECES = [(0, 384), (384, 768), (768, 1152), (1152, 1408), (1408, 1536)]
+GATE_CHUNKS = [(0, 384), (384, 1536)]
+W_CHUNKS = [(0, 3), (3, 12)]
+TOKEN_CUT = 320
+
+
+def tile_moe_pre_lin_none_kernel(tc, xT, w_words, w_scales, gate, offs, pos1, pos2, pos3, out):
+    nc = tc.nc
+    with ExitStack() as ctx:
+        lists = ctx.enter_context(tc.tile_pool(name="lists", bufs=1))
+        keep = ctx.enter_context(tc.tile_pool(name="keep", bufs=1))
+        ring = ctx.enter_context(tc.tile_pool(name="ring", bufs=2))
+        psum = ctx.enter_context(tc.psum_pool(name="psum", bufs=4))
+
+        slot_list = lists.tile([P, S // 16], U16, name="slot_list")
+        back_lists = [lists.tile([P, T // 16], U16, name="back_list%d" % r) for r in range(3)]
+        x_rows = [keep.tile([P, T], F32, name="x_row%d" % j) for j in range(PACK)]
+        gates = [keep.tile([P, b - a], F32, name="gate%d" % a) for a, b in GATE_CHUNKS]
+        w_codes = [keep.tile([P, b - a, 2 * N], U8, name="w_codes%d" % a, align_bytes=64) for a, b in W_CHUNKS]
+        w_plane = keep.tile([P, E, N], U8, name="w_plane", align_bytes=64)
+        y = [keep.tile([P, S], F32, name="y%d" % h) for h in range(2)]
+
+        x_hbm = xT.rearrange("(p j) t -> p j t", j=PACK)
+        gate_hbm = gate.rearrange("(p j) s -> p j s", j=PACK)
+        words_hbm = w_words.rearrange("e a p b -> p (e a) b")
+        scales_hbm = w_scales.rearrange("e a q n -> q (e a) n")
+
+        def load_gate(i):
+            a, b = GATE_CHUNKS[i]
+            nc.sync.dma_start(gates[i][:], gate_hbm[:, 0, a:b])
+
+        def load_words(i):
+            a, b = W_CHUNKS[i]
+            nc.sync.dma_start(w_codes[i][:].bitcast(I32), words_hbm[:, a:b, :].bitcast(I32))
+
+        nc.vector.memset(w_plane[:].bitcast(I32), 0)
+        nc.sync.dma_start(x_rows[0][:], x_hbm[:, 0, :])
+        nc.sync.dma_start(slot_list[:], offs)
+        load_gate(0)
+        for j in range(1, PACK):
+            nc.sync.dma_start(x_rows[j][:], x_hbm[:, j, :])
+        load_gate(1)
+        for q in range(4):
+            nc.sync.dma_start(w_plane[32 * q : 32 * q + 4, :, :].bitcast(I32), scales_hbm[4 * q : 4 * q + 4, :, :].bitcast(I32))
+        load_words(0)
+        load_words(1)
+        for tile, pos in zip(back_lists, (pos1, pos2, pos3)):
+            nc.sync.dma_start(tile[:], pos)
+
+        rounded = {}
+        gathered = {}
+
+        def gather(i):
+            a, b = PIECES[i]
+            g = [n for n, (lo, hi) in enumerate(GATE_CHUNKS) if lo <= a < hi][0]
+            lo = GATE_CHUNKS[g][0]
+            gathered[i] = ring.tile([P, PACK, b - a], F32, name="gathered")
+            for j in range(PACK):
+                nc.vector.tensor_tensor(
+                    gathered[i][:, j, :],
+                    x_rows[j][:].indirect(slot_list[:, a // 16 : b // 16]),
+                    gates[g][:, a - lo : b - lo],
+                    MULT,
+                )
+
+        def interleave(i, on_vector):
+            a, b = PIECES[i]
+            rounded[i] = keep.tile([P, b - a, PACK], BF16, name="rounded%d" % i, align_bytes=64)
+            src = gathered[i][:].rearrange("p j (c s) -> p c j s", s=4)
+            dst = rounded[i][:].rearrange("p (c s) j -> p c j s", s=4)
+            if on_vector:
+                nc.vector.tensor_copy(dst, src)
+            else:
+                nc.scalar.copy(dst, src)
+
+        codes = {}
+        planes = {}
+
+        def quantize(i):
+            a, b = PIECES[i]
+            codes[i] = keep.tile([P, b - a], U32, name="codes%d" % i, align_bytes=64)
+            planes[i] = keep.tile([P, b - a], U8, name="plane%d" % i, align_bytes=64)
+            for lo in range(0, b - a, 256):
+                hi = min(lo + 256, b - a)
+                nc.vector.quantize_mx(
+                    out=codes[i][:, lo:hi].bitcast(FP8X4),
+                    scales=planes[i][:, lo:hi],
+                    in_=rounded[i][:, lo:hi, :].rearrange("p s j -> p (s j)"),
+                )
+
+        def multiply(pieces, h):
+            first, end = PIECES[pieces[0]][0], PIECES[pieces[-1]][1]
+            acc = psum.tile([P, 384], F32, name="acc%d" % h)
+            for i in pieces:
+                a, b = PIECES[i]
+                for e in range(a // C, b // C):
+                    w = [n for n, (lo, hi) in enumerate(W_CHUNKS) if lo <= e < hi][0]
+                    cols = slice(e * C - a, (e + 1) * C - a)
+                    nc.tensor.matmul_mx(
+                        out=acc[:, e * C - first : (e + 1) * C - first],
+                        lhsT=w_codes[w][:, e - W_CHUNKS[w][0], 2 * P * h : 2 * P * (h + 1)].bitcast(FP4X4),
+                        lhsT_scale=w_plane[:, e, P * h : P * (h + 1)],
+                        rhs=codes[i][:, cols].bitcast(FP8X4),
+                        rhs_scale=planes[i][:, cols],
+                        start=True,
+                        stop=True,
+                    )
+            nc.scalar.copy(y[h][:, first:end], acc[:, : end - first])
+
+        last = len(PIECES) - 1
+        gather(0)
+        interleave(0, False)
+        for i in range(1, last):
+            gather(i)
+            interleave(i, False)
+            quantize(i - 1)
+            multiply([i - 1], 0)
+            multiply([i - 1], 1)
+        gather(last)
+        quantize(last - 1)
+        multiply([last - 1], 0)
+        interleave(last, True)
+        quantize(last)
+        multiply([last], 0)
+        multiply([last - 1, last], 1)
+
+        back = [[keep.tile([P, T], F32, name="back%d_%d" % (h, r)) for r in range(3)] for h in range(2)]
+        pair = [keep.tile([P, T], F32, name="pair%d" % h) for h in range(2)]
+        total = [keep.tile([P, T], F32, name="total%d" % h) for h in range(2)]
+
+        def fetch(h, r, a, b):
+            nc.vector.tensor_copy(back[h][r][:, a:b], y[h][:].indirect(back_lists[r][:, a // 16 : b // 16]))
+
+        fetch(0, 0, 0, T)
+        fetch(0, 1, 0, T)
+        nc.gpsimd.tensor_tensor(pair[0][:], back[0][0][:], back[0][1][:], ADD)
+        fetch(0, 2, 0, T)
+        nc.gpsimd.tensor_tensor(total[0][:], pair[0][:], back[0][2][:], ADD)
+        nc.sync.dma_start(out[0:P, :], total[0][:])
+        cuts = [(0, TOKEN_CUT), (TOKEN_CUT, T)]
+        fetch(1, 0, 0, T)
+        for a, b in cuts:
+            fetch(1, 1, a, b)
+            nc.gpsimd.tensor_tensor(pair[1][:, a:b], back[1][0][:, a:b], back[1][1][:, a:b], ADD)
+        for a, b in cuts:
+            fetch(1, 2, a, b)
+        for (a, b), queue in zip(cuts, (nc.sync, nc.scalar)):
+            nc.vector.tensor_tensor(total[1][:, a:b], pair[1][:, a:b], back[1][2][:, a:b], ADD)
+            queue.dma_start(out[P : 2 * P, a:b], total[1][:, a:b])

@@ -20,9 +20,10 @@ FP4X4 = mybir.dt.float4_e2m1fn_x4
 MULT = mybir.AluOpType.mult
 ADD = mybir.AluOpType.add
 
-PIECES = [(0, 384), (384, 768), (768, 1152), (1152, 1408), (1408, 1536)]
-GATE_CHUNKS = [(0, 384), (384, 1536)]
-W_CHUNKS = [(0, 3), (3, 12)]
+PIECES = [(0, 640), (640, 1152), (1152, 1408), (1408, 1536)]
+WINDOW = 656
+GATE_CHUNKS = [(0, 192), (192, 640), (640, 1536)]
+W_CHUNKS = [(0, 5), (5, 12)]
 TOKEN_CUT = 320
 
 
@@ -32,12 +33,12 @@ def tile_moe_pre_lin_none_kernel(tc, xT, w_words, w_scales, gate, offs, pos1, po
         lists = ctx.enter_context(tc.tile_pool(name="lists", bufs=1))
         keep = ctx.enter_context(tc.tile_pool(name="keep", bufs=1))
         ring = ctx.enter_context(tc.tile_pool(name="ring", bufs=2))
-        psum = ctx.enter_context(tc.psum_pool(name="psum", bufs=4))
+        psum = ctx.enter_context(tc.psum_pool(name="psum", bufs=8))
 
         slot_list = lists.tile([P, S // 16], U16, name="slot_list")
         back_lists = [lists.tile([P, T // 16], U16, name="back_list%d" % r) for r in range(3)]
-        x_rows = [keep.tile([P, T], F32, name="x_row%d" % j) for j in range(PACK)]
-        gates = [keep.tile([P, b - a], F32, name="gate%d" % a) for a, b in GATE_CHUNKS]
+        x_rows = [keep.tile([P, WINDOW], F32, name="x_row%d" % j) for j in range(PACK)]
+        gates = keep.tile([P, S], F32, name="gates")
         w_codes = [keep.tile([P, b - a, 2 * N], U8, name="w_codes%d" % a, align_bytes=64) for a, b in W_CHUNKS]
         w_plane = keep.tile([P, E, N], U8, name="w_plane", align_bytes=64)
         y = [keep.tile([P, S], F32, name="y%d" % h) for h in range(2)]
@@ -49,19 +50,20 @@ def tile_moe_pre_lin_none_kernel(tc, xT, w_words, w_scales, gate, offs, pos1, po
 
         def load_gate(i):
             a, b = GATE_CHUNKS[i]
-            nc.sync.dma_start(gates[i][:], gate_hbm[:, 0, a:b])
+            nc.sync.dma_start(gates[:, a:b], gate_hbm[:, 0, a:b])
 
         def load_words(i):
             a, b = W_CHUNKS[i]
             nc.sync.dma_start(w_codes[i][:].bitcast(I32), words_hbm[:, a:b, :].bitcast(I32))
 
         nc.vector.memset(w_plane[:].bitcast(I32), 0)
-        nc.sync.dma_start(x_rows[0][:], x_hbm[:, 0, :])
+        nc.sync.dma_start(x_rows[0][:, :T], x_hbm[:, 0, :])
         nc.sync.dma_start(slot_list[:], offs)
         load_gate(0)
-        for j in range(1, PACK):
-            nc.sync.dma_start(x_rows[j][:], x_hbm[:, j, :])
         load_gate(1)
+        for j in range(1, PACK):
+            nc.sync.dma_start(x_rows[j][:, :T], x_hbm[:, j, :])
+        load_gate(2)
         for q in range(4):
             nc.sync.dma_start(w_plane[32 * q : 32 * q + 4, :, :].bitcast(I32), scales_hbm[4 * q : 4 * q + 4, :, :].bitcast(I32))
         load_words(0)
@@ -74,16 +76,16 @@ def tile_moe_pre_lin_none_kernel(tc, xT, w_words, w_scales, gate, offs, pos1, po
 
         def gather(i):
             a, b = PIECES[i]
-            g = [n for n, (lo, hi) in enumerate(GATE_CHUNKS) if lo <= a < hi][0]
-            lo = GATE_CHUNKS[g][0]
             gathered[i] = ring.tile([P, PACK, b - a], F32, name="gathered")
             for j in range(PACK):
-                nc.vector.tensor_tensor(
-                    gathered[i][:, j, :],
-                    x_rows[j][:].indirect(slot_list[:, a // 16 : b // 16]),
-                    gates[g][:, a - lo : b - lo],
-                    MULT,
-                )
+                spans = GATE_CHUNKS[:2] if i == 0 and j == 0 else [(a, b)]
+                for c, d in spans:
+                    nc.vector.tensor_tensor(
+                        gathered[i][:, j, c - a : d - a],
+                        x_rows[j][:].indirect(slot_list[:, c // 16 : d // 16]),
+                        gates[:, c:d],
+                        MULT,
+                    )
 
         def interleave(i, on_vector):
             a, b = PIECES[i]
@@ -98,53 +100,54 @@ def tile_moe_pre_lin_none_kernel(tc, xT, w_words, w_scales, gate, offs, pos1, po
         codes = {}
         planes = {}
 
-        def quantize(i):
+        def quantize(i, spans):
             a, b = PIECES[i]
-            codes[i] = keep.tile([P, b - a], U32, name="codes%d" % i, align_bytes=64)
-            planes[i] = keep.tile([P, b - a], U8, name="plane%d" % i, align_bytes=64)
-            for lo in range(0, b - a, 256):
-                hi = min(lo + 256, b - a)
+            if i not in codes:
+                codes[i] = keep.tile([P, b - a], U32, name="codes%d" % i, align_bytes=64)
+                planes[i] = keep.tile([P, b - a], U8, name="plane%d" % i, align_bytes=64)
+            for lo, hi in spans:
                 nc.vector.quantize_mx(
                     out=codes[i][:, lo:hi].bitcast(FP8X4),
                     scales=planes[i][:, lo:hi],
                     in_=rounded[i][:, lo:hi, :].rearrange("p s j -> p (s j)"),
                 )
 
-        def multiply(pieces, h):
-            first, end = PIECES[pieces[0]][0], PIECES[pieces[-1]][1]
-            acc = psum.tile([P, 384], F32, name="acc%d" % h)
-            for i in pieces:
-                a, b = PIECES[i]
-                for e in range(a // C, b // C):
-                    w = [n for n, (lo, hi) in enumerate(W_CHUNKS) if lo <= e < hi][0]
-                    cols = slice(e * C - a, (e + 1) * C - a)
-                    nc.tensor.matmul_mx(
-                        out=acc[:, e * C - first : (e + 1) * C - first],
-                        lhsT=w_codes[w][:, e - W_CHUNKS[w][0], 2 * P * h : 2 * P * (h + 1)].bitcast(FP4X4),
-                        lhsT_scale=w_plane[:, e, P * h : P * (h + 1)],
-                        rhs=codes[i][:, cols].bitcast(FP8X4),
-                        rhs_scale=planes[i][:, cols],
-                        start=True,
-                        stop=True,
-                    )
+        def multiply(first, end, h):
+            acc = psum.tile([P, 512], F32, name="acc")
+            for e in range(first // C, end // C):
+                i = [n for n, (lo, hi) in enumerate(PIECES) if lo <= e * C < hi][0]
+                w = [n for n, (lo, hi) in enumerate(W_CHUNKS) if lo <= e < hi][0]
+                cols = slice(e * C - PIECES[i][0], (e + 1) * C - PIECES[i][0])
+                nc.tensor.matmul_mx(
+                    out=acc[:, e * C - first : (e + 1) * C - first],
+                    lhsT=w_codes[w][:, e - W_CHUNKS[w][0], 2 * P * h : 2 * P * (h + 1)].bitcast(FP4X4),
+                    lhsT_scale=w_plane[:, e, P * h : P * (h + 1)],
+                    rhs=codes[i][:, cols].bitcast(FP8X4),
+                    rhs_scale=planes[i][:, cols],
+                    start=True,
+                    stop=True,
+                )
             nc.scalar.copy(y[h][:, first:end], acc[:, : end - first])
 
-        last = len(PIECES) - 1
         gather(0)
         interleave(0, False)
-        for i in range(1, last):
-            gather(i)
-            interleave(i, False)
-            quantize(i - 1)
-            multiply([i - 1], 0)
-            multiply([i - 1], 1)
-        gather(last)
-        quantize(last - 1)
-        multiply([last - 1], 0)
-        interleave(last, True)
-        quantize(last)
-        multiply([last], 0)
-        multiply([last - 1, last], 1)
+        gather(1)
+        interleave(1, False)
+        quantize(0, [(0, 512), (512, 640)])
+        multiply(0, 512, 0)
+        gather(2)
+        interleave(2, False)
+        quantize(1, [(0, 512)])
+        multiply(512, 1024, 0)
+        gather(3)
+        quantize(2, [(0, 128)])
+        interleave(3, True)
+        quantize(2, [(128, 256)])
+        multiply(1024, 1408, 0)
+        quantize(3, [(0, 128)])
+        multiply(1408, 1536, 0)
+        for first in range(0, S, 512):
+            multiply(first, first + 512, 1)
 
         back = [[keep.tile([P, T], F32, name="back%d_%d" % (h, r)) for r in range(3)] for h in range(2)]
         pair = [keep.tile([P, T], F32, name="pair%d" % h) for h in range(2)]

@@ -20,11 +20,13 @@ FP4X4 = mybir.dt.float4_e2m1fn_x4
 MULT = mybir.AluOpType.mult
 ADD = mybir.AluOpType.add
 
-PIECES = [(0, 640), (640, 1152), (1152, 1408), (1408, 1536)]
-WINDOW = 656
-GATE_CHUNKS = [(0, 192), (192, 640), (640, 1536)]
-W_CHUNKS = [(0, 5), (5, 12)]
-TOKEN_CUT = 320
+PIECES = [(0, 704), (704, 1152), (1152, 1408), (1408, 1536)]
+WINDOW = 720
+GATE_CHUNKS = [(0, 192), (192, 704), (704, 1536)]
+W_CHUNKS = [(0, 4), (4, 12)]
+TOKEN_CUT = 384
+BANKS = [(0, 4), (4, 8), (8, 10), (10, 12)]
+SPANS = [(0, 512), (512, 1024), (1024, 1280), (1280, 1408), (1408, 1536)]
 
 
 def tile_moe_pre_lin_none_kernel(tc, xT, w_words, w_scales, gate, offs, pos1, pos2, pos3, out):
@@ -71,12 +73,15 @@ def tile_moe_pre_lin_none_kernel(tc, xT, w_words, w_scales, gate, offs, pos1, po
         for tile, pos in zip(back_lists, (pos1, pos2, pos3)):
             nc.sync.dma_start(tile[:], pos)
 
-        rounded = {}
+        last = len(PIECES) - 1
+        tail = PIECES[last][0]
+        rounded = keep.tile([P, tail, PACK], BF16, name="rounded", align_bytes=64)
         gathered = {}
+        rounded_last = []
 
         def gather(i):
             a, b = PIECES[i]
-            gathered[i] = ring.tile([P, PACK, b - a], F32, name="gathered")
+            gathered[i] = ring.tile([P, PACK, b - a], F32, name="gathered", align_bytes=64)
             for j in range(PACK):
                 spans = GATE_CHUNKS[:2] if i == 0 and j == 0 else [(a, b)]
                 for c, d in spans:
@@ -87,88 +92,79 @@ def tile_moe_pre_lin_none_kernel(tc, xT, w_words, w_scales, gate, offs, pos1, po
                         MULT,
                     )
 
-        def interleave(i, on_vector):
+        def interleave(i):
             a, b = PIECES[i]
-            rounded[i] = keep.tile([P, b - a, PACK], BF16, name="rounded%d" % i, align_bytes=64)
             src = gathered[i][:].rearrange("p j (c s) -> p c j s", s=4)
-            dst = rounded[i][:].rearrange("p (c s) j -> p c j s", s=4)
-            if on_vector:
-                nc.vector.tensor_copy(dst, src)
+            if i == last:
+                rounded_last.append(ring.tile([P, b - a, PACK], BF16, name="gathered", align_bytes=64))
+                nc.vector.tensor_copy(rounded_last[0][:].rearrange("p (c s) j -> p c j s", s=4), src)
             else:
-                nc.scalar.copy(dst, src)
+                nc.scalar.copy(rounded[:, a:b, :].rearrange("p (c s) j -> p c j s", s=4), src)
 
         codes = {}
         planes = {}
 
-        def quantize(i, spans):
-            a, b = PIECES[i]
-            if i not in codes:
-                codes[i] = keep.tile([P, b - a], U32, name="codes%d" % i, align_bytes=64)
-                planes[i] = keep.tile([P, b - a], U8, name="plane%d" % i, align_bytes=64)
-            for lo, hi in spans:
-                nc.vector.quantize_mx(
-                    out=codes[i][:, lo:hi].bitcast(FP8X4),
-                    scales=planes[i][:, lo:hi],
-                    in_=rounded[i][:, lo:hi, :].rearrange("p s j -> p (s j)"),
-                )
+        def quantize(n):
+            a, b = SPANS[n]
+            codes[n] = keep.tile([P, b - a], U32, name="codes%d" % n, align_bytes=64)
+            planes[n] = keep.tile([P, b - a], U8, name="plane%d" % n, align_bytes=64)
+            src = rounded_last[0][:, a - tail : b - tail, :] if a >= tail else rounded[:, a:b, :]
+            nc.vector.quantize_mx(out=codes[n][:].bitcast(FP8X4), scales=planes[n][:], in_=src.rearrange("p s j -> p (s j)"))
 
-        def multiply(first, end, h):
-            acc = psum.tile([P, 512], F32, name="acc")
-            for e in range(first // C, end // C):
-                i = [n for n, (lo, hi) in enumerate(PIECES) if lo <= e * C < hi][0]
-                w = [n for n, (lo, hi) in enumerate(W_CHUNKS) if lo <= e < hi][0]
-                cols = slice(e * C - PIECES[i][0], (e + 1) * C - PIECES[i][0])
-                nc.tensor.matmul_mx(
-                    out=acc[:, e * C - first : (e + 1) * C - first],
-                    lhsT=w_codes[w][:, e - W_CHUNKS[w][0], 2 * P * h : 2 * P * (h + 1)].bitcast(FP4X4),
-                    lhsT_scale=w_plane[:, e, P * h : P * (h + 1)],
-                    rhs=codes[i][:, cols].bitcast(FP8X4),
-                    rhs_scale=planes[i][:, cols],
-                    start=True,
-                    stop=True,
-                )
-            nc.scalar.copy(y[h][:, first:end], acc[:, : end - first])
+        def bank(b, on_vector=()):
+            first, end = BANKS[b]
+            for h in range(2):
+                acc = psum.tile([P, 512], F32, name="acc")
+                for e in range(first, end):
+                    n = [n for n, (lo, hi) in enumerate(SPANS) if lo <= e * C < hi][0]
+                    w = [n for n, (lo, hi) in enumerate(W_CHUNKS) if lo <= e < hi][0]
+                    cols = slice(e * C - SPANS[n][0], (e + 1) * C - SPANS[n][0])
+                    nc.tensor.matmul_mx(
+                        out=acc[:, (e - first) * C : (e - first + 1) * C],
+                        lhsT=w_codes[w][:, e - W_CHUNKS[w][0], 2 * P * h : 2 * P * (h + 1)].bitcast(FP4X4),
+                        lhsT_scale=w_plane[:, e, P * h : P * (h + 1)],
+                        rhs=codes[n][:, cols].bitcast(FP8X4),
+                        rhs_scale=planes[n][:, cols],
+                        start=True,
+                        stop=True,
+                    )
+                if h in on_vector:
+                    nc.vector.tensor_copy(y[h][:, first * C : end * C], acc[:, : (end - first) * C])
+                else:
+                    nc.scalar.copy(y[h][:, first * C : end * C], acc[:, : (end - first) * C])
 
         gather(0)
-        interleave(0, False)
+        interleave(0)
         gather(1)
-        interleave(1, False)
-        quantize(0, [(0, 512), (512, 640)])
-        multiply(0, 512, 0)
+        interleave(1)
+        quantize(0)
+        bank(0)
         gather(2)
-        interleave(2, False)
-        quantize(1, [(0, 512)])
-        multiply(512, 1024, 0)
+        interleave(2)
+        quantize(1)
+        bank(1)
         gather(3)
-        quantize(2, [(0, 128)])
-        interleave(3, True)
-        quantize(2, [(128, 256)])
-        multiply(1024, 1408, 0)
-        quantize(3, [(0, 128)])
-        multiply(1408, 1536, 0)
-        for first in range(0, S, 512):
-            multiply(first, first + 512, 1)
+        quantize(2)
+        interleave(3)
+        quantize(3)
+        quantize(4)
+        bank(2, (1,))
+        bank(3)
 
-        back = [[keep.tile([P, T], F32, name="back%d_%d" % (h, r)) for r in range(3)] for h in range(2)]
-        pair = [keep.tile([P, T], F32, name="pair%d" % h) for h in range(2)]
-        total = [keep.tile([P, T], F32, name="total%d" % h) for h in range(2)]
+        sums = [[keep.tile([P, T], F32, name="sum%d_%d" % (h, r)) for r in range(3)] for h in range(2)]
 
         def fetch(h, r, a, b):
-            nc.vector.tensor_copy(back[h][r][:, a:b], y[h][:].indirect(back_lists[r][:, a // 16 : b // 16]))
+            picked = y[h][:].indirect(back_lists[r][:, a // 16 : b // 16])
+            if r == 0:
+                nc.vector.tensor_copy(sums[h][0][:, a:b], picked)
+            else:
+                nc.vector.tensor_tensor(sums[h][r][:, a:b], picked, sums[h][r - 1][:, a:b], ADD)
 
-        fetch(0, 0, 0, T)
-        fetch(0, 1, 0, T)
-        nc.gpsimd.tensor_tensor(pair[0][:], back[0][0][:], back[0][1][:], ADD)
+        for r in range(2):
+            for h in range(2):
+                fetch(h, r, 0, T)
         fetch(0, 2, 0, T)
-        nc.gpsimd.tensor_tensor(total[0][:], pair[0][:], back[0][2][:], ADD)
-        nc.sync.dma_start(out[0:P, :], total[0][:])
-        cuts = [(0, TOKEN_CUT), (TOKEN_CUT, T)]
-        fetch(1, 0, 0, T)
-        for a, b in cuts:
-            fetch(1, 1, a, b)
-            nc.gpsimd.tensor_tensor(pair[1][:, a:b], back[1][0][:, a:b], back[1][1][:, a:b], ADD)
-        for a, b in cuts:
+        nc.sync.dma_start(out[0:P, :], sums[0][2][:])
+        for a, b in [(0, TOKEN_CUT), (TOKEN_CUT, T)]:
             fetch(1, 2, a, b)
-        for (a, b), queue in zip(cuts, (nc.sync, nc.scalar)):
-            nc.vector.tensor_tensor(total[1][:, a:b], pair[1][:, a:b], back[1][2][:, a:b], ADD)
-            queue.dma_start(out[P : 2 * P, a:b], total[1][:, a:b])
+            nc.sync.dma_start(out[P : 2 * P, a:b], sums[1][2][:, a:b])

@@ -20,12 +20,12 @@ FP4X4 = mybir.dt.float4_e2m1fn_x4
 MULT = mybir.AluOpType.mult
 ADD = mybir.AluOpType.add
 
-PIECES = [(0, 704), (704, 1152), (1152, 1408), (1408, 1536)]
-WINDOW = 720
-GATE_CHUNKS = [(0, 192), (192, 704), (704, 1536)]
+PIECES = [(0, 768), (768, 1152), (1152, 1408), (1408, 1536)]
+WINDOW = 784
+GATE_CHUNKS = [(0, 192), (192, 768), (768, 1536)]
 W_CHUNKS = [(0, 4), (4, 12)]
 TOKEN_CUT = 384
-BANKS = [(0, 4), (4, 8), (8, 10), (10, 12)]
+BANKS = [(0, 4), (4, 8), (8, 10), (10, 12), (10, 11), (11, 12)]
 SPANS = [(0, 512), (512, 1024), (1024, 1280), (1280, 1408), (1408, 1536)]
 
 
@@ -34,7 +34,6 @@ def tile_moe_pre_lin_none_kernel(tc, xT, w_words, w_scales, gate, offs, pos1, po
     with ExitStack() as ctx:
         lists = ctx.enter_context(tc.tile_pool(name="lists", bufs=1))
         keep = ctx.enter_context(tc.tile_pool(name="keep", bufs=1))
-        ring = ctx.enter_context(tc.tile_pool(name="ring", bufs=2))
         psum = ctx.enter_context(tc.psum_pool(name="psum", bufs=8))
 
         slot_list = lists.tile([P, S // 16], U16, name="slot_list")
@@ -42,8 +41,8 @@ def tile_moe_pre_lin_none_kernel(tc, xT, w_words, w_scales, gate, offs, pos1, po
         x_rows = [keep.tile([P, WINDOW], F32, name="x_row%d" % j) for j in range(PACK)]
         gates = keep.tile([P, S], F32, name="gates")
         w_codes = [keep.tile([P, b - a, 2 * N], U8, name="w_codes%d" % a, align_bytes=64) for a, b in W_CHUNKS]
-        w_plane = keep.tile([P, E, N], U8, name="w_plane", align_bytes=64)
-        y = [keep.tile([P, S], F32, name="y%d" % h) for h in range(2)]
+        w_planes = [keep.tile([P, b - a, N], U8, name="w_plane%d" % a, align_bytes=64) for a, b in W_CHUNKS]
+        y = [keep.tile([P, width], F32, name="y%d" % h) for h, width in enumerate((S, 512 + PACK * (PIECES[1][1] - PIECES[1][0])))]
 
         x_hbm = xT.rearrange("(p j) t -> p j t", j=PACK)
         gate_hbm = gate.rearrange("(p j) s -> p j s", j=PACK)
@@ -56,9 +55,12 @@ def tile_moe_pre_lin_none_kernel(tc, xT, w_words, w_scales, gate, offs, pos1, po
 
         def load_words(i):
             a, b = W_CHUNKS[i]
+            for q in range(4):
+                nc.sync.dma_start(w_planes[i][32 * q : 32 * q + 4, :, :].bitcast(I32), scales_hbm[4 * q : 4 * q + 4, a:b, :].bitcast(I32))
             nc.sync.dma_start(w_codes[i][:].bitcast(I32), words_hbm[:, a:b, :].bitcast(I32))
 
-        nc.vector.memset(w_plane[:].bitcast(I32), 0)
+        for plane in w_planes:
+            nc.vector.memset(plane[:].bitcast(I32), 0)
         nc.sync.dma_start(x_rows[0][:, :T], x_hbm[:, 0, :])
         nc.sync.dma_start(slot_list[:], offs)
         load_gate(0)
@@ -66,40 +68,48 @@ def tile_moe_pre_lin_none_kernel(tc, xT, w_words, w_scales, gate, offs, pos1, po
         for j in range(1, PACK):
             nc.sync.dma_start(x_rows[j][:, :T], x_hbm[:, j, :])
         load_gate(2)
-        for q in range(4):
-            nc.sync.dma_start(w_plane[32 * q : 32 * q + 4, :, :].bitcast(I32), scales_hbm[4 * q : 4 * q + 4, :, :].bitcast(I32))
         load_words(0)
         load_words(1)
         for tile, pos in zip(back_lists, (pos1, pos2, pos3)):
             nc.sync.dma_start(tile[:], pos)
 
-        last = len(PIECES) - 1
-        tail = PIECES[last][0]
-        rounded = keep.tile([P, tail, PACK], BF16, name="rounded", align_bytes=64)
-        gathered = {}
-        rounded_last = []
+        (a0, b0), (a1, b1), (a2, b2), (a3, b3) = PIECES
+        stage = keep.tile([P, PACK * b0], F32, name="stage", align_bytes=64)
 
-        def gather(i):
-            a, b = PIECES[i]
-            gathered[i] = ring.tile([P, PACK, b - a], F32, name="gathered", align_bytes=64)
-            for j in range(PACK):
-                spans = GATE_CHUNKS[:2] if i == 0 and j == 0 else [(a, b)]
-                for c, d in spans:
-                    nc.vector.tensor_tensor(
-                        gathered[i][:, j, c - a : d - a],
-                        x_rows[j][:].indirect(slot_list[:, c // 16 : d // 16]),
-                        gates[:, c:d],
-                        MULT,
-                    )
+        def rows(tile, start, slots):
+            return tile[:, start : start + PACK * slots].rearrange("p (j s) -> p j s", j=PACK)
 
-        def interleave(i):
-            a, b = PIECES[i]
-            src = gathered[i][:].rearrange("p j (c s) -> p c j s", s=4)
-            if i == last:
-                rounded_last.append(ring.tile([P, b - a, PACK], BF16, name="gathered", align_bytes=64))
-                nc.vector.tensor_copy(rounded_last[0][:].rearrange("p (c s) j -> p c j s", s=4), src)
+        gathered = {
+            a0: rows(stage, 0, b0),
+            a1: rows(y[1], 512, b1 - a1),
+            a2: rows(stage, 0, b2 - a2),
+            a3: rows(y[1], 512, b3 - a3),
+        }
+        rounded = {0: keep.tile([P, a3, PACK], BF16, name="rounded", align_bytes=64)[:]}
+
+        def rounded_slots(a, b):
+            first = max(f for f in rounded if f <= a)
+            return rounded[first][:, a - first : b - first, :]
+
+        def gather(first, js, a, b):
+            for j in js:
+                nc.vector.tensor_tensor(
+                    gathered[first][:, j, a - first : b - first],
+                    x_rows[j][:].indirect(slot_list[:, a // 16 : b // 16]),
+                    gates[:, a:b],
+                    MULT,
+                )
+
+        def interleave(a, b):
+            first = max(f for f in gathered if f <= a)
+            src = gathered[first][:, :, a - first : b - first].rearrange("p j (c s) -> p c j s", s=4)
+            if a == a3:
+                rounded[a] = stage[:, : 2 * (b - a)].bitcast(BF16).rearrange("p (s j) -> p s j", j=PACK)
+            dst = rounded_slots(a, b).rearrange("p (c s) j -> p c j s", s=4)
+            if a == a3:
+                nc.vector.tensor_copy(dst, src)
             else:
-                nc.scalar.copy(rounded[:, a:b, :].rearrange("p (c s) j -> p c j s", s=4), src)
+                nc.scalar.copy(dst, src)
 
         codes = {}
         planes = {}
@@ -108,48 +118,65 @@ def tile_moe_pre_lin_none_kernel(tc, xT, w_words, w_scales, gate, offs, pos1, po
             a, b = SPANS[n]
             codes[n] = keep.tile([P, b - a], U32, name="codes%d" % n, align_bytes=64)
             planes[n] = keep.tile([P, b - a], U8, name="plane%d" % n, align_bytes=64)
-            src = rounded_last[0][:, a - tail : b - tail, :] if a >= tail else rounded[:, a:b, :]
+            src = rounded_slots(a, b)
             nc.vector.quantize_mx(out=codes[n][:].bitcast(FP8X4), scales=planes[n][:], in_=src.rearrange("p s j -> p (s j)"))
 
-        def bank(b, on_vector=()):
-            first, end = BANKS[b]
-            for h in range(2):
-                acc = psum.tile([P, 512], F32, name="acc")
-                for e in range(first, end):
-                    n = [n for n, (lo, hi) in enumerate(SPANS) if lo <= e * C < hi][0]
-                    w = [n for n, (lo, hi) in enumerate(W_CHUNKS) if lo <= e < hi][0]
-                    cols = slice(e * C - SPANS[n][0], (e + 1) * C - SPANS[n][0])
-                    nc.tensor.matmul_mx(
-                        out=acc[:, (e - first) * C : (e - first + 1) * C],
-                        lhsT=w_codes[w][:, e - W_CHUNKS[w][0], 2 * P * h : 2 * P * (h + 1)].bitcast(FP4X4),
-                        lhsT_scale=w_plane[:, e, P * h : P * (h + 1)],
-                        rhs=codes[n][:, cols].bitcast(FP8X4),
-                        rhs_scale=planes[n][:, cols],
-                        start=True,
-                        stop=True,
-                    )
-                if h in on_vector:
-                    nc.vector.tensor_copy(y[h][:, first * C : end * C], acc[:, : (end - first) * C])
-                else:
-                    nc.scalar.copy(y[h][:, first * C : end * C], acc[:, : (end - first) * C])
+        acc = {}
 
-        gather(0)
-        interleave(0)
-        gather(1)
-        interleave(1)
+        def multiply(b, h):
+            first, end = BANKS[b]
+            acc[b, h] = psum.tile([P, 512], F32, name="acc")
+            for e in range(first, end):
+                n = [n for n, (lo, hi) in enumerate(SPANS) if lo <= e * C < hi][0]
+                w = [n for n, (lo, hi) in enumerate(W_CHUNKS) if lo <= e < hi][0]
+                cols = slice(e * C - SPANS[n][0], (e + 1) * C - SPANS[n][0])
+                nc.tensor.matmul_mx(
+                    out=acc[b, h][:, (e - first) * C : (e - first + 1) * C],
+                    lhsT=w_codes[w][:, e - W_CHUNKS[w][0], 2 * P * h : 2 * P * (h + 1)].bitcast(FP4X4),
+                    lhsT_scale=w_planes[w][:, e - W_CHUNKS[w][0], P * h : P * (h + 1)],
+                    rhs=codes[n][:, cols].bitcast(FP8X4),
+                    rhs_scale=planes[n][:, cols],
+                    start=True,
+                    stop=True,
+                )
+
+        def empty(b, h, on_vector=False):
+            first, end = BANKS[b]
+            if on_vector:
+                nc.vector.tensor_copy(y[h][:, first * C : end * C], acc[b, h][:, : (end - first) * C])
+            else:
+                nc.scalar.copy(y[h][:, first * C : end * C], acc[b, h][:, : (end - first) * C])
+
+        def bank(b):
+            for h in range(2):
+                multiply(b, h)
+                empty(b, h)
+
+        gather(a0, [0], *GATE_CHUNKS[0])
+        gather(a0, [0], *GATE_CHUNKS[1])
+        gather(a0, [1, 2, 3], a0, b0)
+        interleave(a0, 512)
+        interleave(512, b0)
+        gather(a1, range(PACK), a1, b1)
+        interleave(a1, b1)
         quantize(0)
         bank(0)
-        gather(2)
-        interleave(2)
+        gather(a2, range(PACK), a2, b2)
+        interleave(a2, b2)
         quantize(1)
-        bank(1)
-        gather(3)
+        multiply(1, 0)
+        empty(1, 0)
+        multiply(1, 1)
+        gather(a3, range(PACK), a3, b3)
         quantize(2)
-        interleave(3)
+        interleave(a3, b3)
         quantize(3)
         quantize(4)
-        bank(2, (1,))
-        bank(3)
+        empty(1, 1, True)
+        bank(2)
+        for b, h in ((4, 0), (5, 0), (3, 1)):
+            multiply(b, h)
+            empty(b, h)
 
         sums = [[keep.tile([P, T], F32, name="sum%d_%d" % (h, r)) for r in range(3)] for h in range(2)]
 

@@ -20,9 +20,9 @@ FP4X4 = mybir.dt.float4_e2m1fn_x4
 MULT = mybir.AluOpType.mult
 ADD = mybir.AluOpType.add
 
-PIECES = [(0, 768), (768, 1152), (1152, 1408), (1408, 1536)]
+PIECES = [(0, 768), (768, 1216), (1216, 1408), (1408, 1536)]
 WINDOW = 784
-GATE_CHUNKS = [(0, 192), (192, 768), (768, 1536)]
+GATE_CHUNKS = [(0, 256), (256, 768), (768, 1536)]
 W_CHUNKS = [(0, 4), (4, 12)]
 TOKEN_CUT = 384
 BANKS = [(0, 4), (4, 8), (8, 10), (10, 12), (10, 11), (11, 12)]
@@ -42,7 +42,7 @@ def tile_moe_pre_lin_none_kernel(tc, xT, w_words, w_scales, gate, offs, pos1, po
         gates = keep.tile([P, S], F32, name="gates")
         w_codes = [keep.tile([P, b - a, 2 * N], U8, name="w_codes%d" % a, align_bytes=64) for a, b in W_CHUNKS]
         w_planes = [keep.tile([P, b - a, N], U8, name="w_plane%d" % a, align_bytes=64) for a, b in W_CHUNKS]
-        y = [keep.tile([P, width], F32, name="y%d" % h) for h, width in enumerate((S, 512 + PACK * (PIECES[1][1] - PIECES[1][0])))]
+        y = [keep.tile([P, S], F32, name="y%d" % h) for h in range(2)]
 
         x_hbm = xT.rearrange("(p j) t -> p j t", j=PACK)
         gate_hbm = gate.rearrange("(p j) s -> p j s", j=PACK)
@@ -74,16 +74,16 @@ def tile_moe_pre_lin_none_kernel(tc, xT, w_words, w_scales, gate, offs, pos1, po
             nc.sync.dma_start(tile[:], pos)
 
         (a0, b0), (a1, b1), (a2, b2), (a3, b3) = PIECES
-        stage = keep.tile([P, PACK * b0], F32, name="stage", align_bytes=64)
+        stride = (PACK * b0 - (b2 - a2)) // 2
+        stage = keep.tile([P, PACK * stride], F32, name="stage", align_bytes=64)
 
         def rows(tile, start, slots):
             return tile[:, start : start + PACK * slots].rearrange("p (j s) -> p j s", j=PACK)
 
         gathered = {
             a0: rows(stage, 0, b0),
-            a1: rows(y[1], 512, b1 - a1),
-            a2: rows(stage, 0, b2 - a2),
-            a3: rows(y[1], 512, b3 - a3),
+            a1: rows(stage, PACK * b0, b1 - a1),
+            a2: rows(stage, 0, stride),
         }
         rounded = {0: keep.tile([P, a3, PACK], BF16, name="rounded", align_bytes=64)[:]}
 
@@ -104,7 +104,7 @@ def tile_moe_pre_lin_none_kernel(tc, xT, w_words, w_scales, gate, offs, pos1, po
             first = max(f for f in gathered if f <= a)
             src = gathered[first][:, :, a - first : b - first].rearrange("p j (c s) -> p c j s", s=4)
             if a == a3:
-                rounded[a] = stage[:, : 2 * (b - a)].bitcast(BF16).rearrange("p (s j) -> p s j", j=PACK)
+                rounded[a] = stage[:, stride + a3 - a2 - 2 * (b - a) : stride + a3 - a2].bitcast(BF16).rearrange("p (s j) -> p s j", j=PACK)
             dst = rounded_slots(a, b).rearrange("p (c s) j -> p c j s", s=4)
             if a == a3:
                 nc.vector.tensor_copy(dst, src)
@@ -161,19 +161,20 @@ def tile_moe_pre_lin_none_kernel(tc, xT, w_words, w_scales, gate, offs, pos1, po
         interleave(a1, b1)
         quantize(0)
         bank(0)
-        gather(a2, range(PACK), a2, b2)
+        gather(a2, [0, 1], a2, b3)
+        gather(a2, [2, 3], a2, b2)
         interleave(a2, b2)
         quantize(1)
-        multiply(1, 0)
-        empty(1, 0)
-        multiply(1, 1)
-        gather(a3, range(PACK), a3, b3)
+        bank(1)
+        gather(a2, [2, 3], a3, b3)
         quantize(2)
         interleave(a3, b3)
         quantize(3)
         quantize(4)
-        empty(1, 1, True)
-        bank(2)
+        multiply(2, 0)
+        empty(2, 0)
+        multiply(2, 1)
+        empty(2, 1, True)
         for b, h in ((4, 0), (5, 0), (3, 1)):
             multiply(b, h)
             empty(b, h)

@@ -25,8 +25,8 @@ WINDOW = 784
 GATE_CHUNKS = [(0, 256), (256, 768), (768, 1536)]
 W_CHUNKS = [(0, 4), (4, 12)]
 TOKEN_CUT = 384
-BANKS = [(0, 4), (4, 8), (8, 10), (10, 12), (10, 11), (11, 12)]
-SPANS = [(0, 512), (512, 1024), (1024, 1280), (1280, 1408), (1408, 1536)]
+SPANS = [(0, 512)] + [(e * C, (e + 1) * C) for e in range(4, E)]
+TAIL_AT, TAIL_PITCH = 768, 384
 
 
 def tile_moe_pre_lin_none_kernel(tc, xT, w_words, w_scales, gate, offs, pos1, pos2, pos3, out):
@@ -34,7 +34,7 @@ def tile_moe_pre_lin_none_kernel(tc, xT, w_words, w_scales, gate, offs, pos1, po
     with ExitStack() as ctx:
         lists = ctx.enter_context(tc.tile_pool(name="lists", bufs=1))
         keep = ctx.enter_context(tc.tile_pool(name="keep", bufs=1))
-        psum = ctx.enter_context(tc.psum_pool(name="psum", bufs=8))
+        psum = ctx.enter_context(tc.psum_pool(name="psum", bufs=1))
 
         slot_list = lists.tile([P, S // 16], U16, name="slot_list")
         back_lists = [lists.tile([P, T // 16], U16, name="back_list%d" % r) for r in range(3)]
@@ -42,7 +42,7 @@ def tile_moe_pre_lin_none_kernel(tc, xT, w_words, w_scales, gate, offs, pos1, po
         gates = keep.tile([P, S], F32, name="gates")
         w_codes = [keep.tile([P, b - a, 2 * N], U8, name="w_codes%d" % a, align_bytes=64) for a, b in W_CHUNKS]
         w_planes = [keep.tile([P, b - a, N], U8, name="w_plane%d" % a, align_bytes=64) for a, b in W_CHUNKS]
-        y = [keep.tile([P, S], F32, name="y%d" % h) for h in range(2)]
+        y = [keep.tile([P, 2 * S], F32, name="y0", align_bytes=64), keep.tile([P, S], F32, name="y1")]
 
         x_hbm = xT.rearrange("(p j) t -> p j t", j=PACK)
         gate_hbm = gate.rearrange("(p j) s -> p j s", j=PACK)
@@ -74,22 +74,13 @@ def tile_moe_pre_lin_none_kernel(tc, xT, w_words, w_scales, gate, offs, pos1, po
             nc.sync.dma_start(tile[:], pos)
 
         (a0, b0), (a1, b1), (a2, b2), (a3, b3) = PIECES
-        stride = (PACK * b0 - (b2 - a2)) // 2
-        stage = keep.tile([P, PACK * stride], F32, name="stage", align_bytes=64)
+        stage = keep.tile([P, PACK * (b1 - a1)], F32, name="stage", align_bytes=64)
 
         def rows(tile, start, slots):
             return tile[:, start : start + PACK * slots].rearrange("p (j s) -> p j s", j=PACK)
 
-        gathered = {
-            a0: rows(stage, 0, b0),
-            a1: rows(stage, PACK * b0, b1 - a1),
-            a2: rows(stage, 0, stride),
-        }
-        rounded = {0: keep.tile([P, a3, PACK], BF16, name="rounded", align_bytes=64)[:]}
-
-        def rounded_slots(a, b):
-            first = max(f for f in rounded if f <= a)
-            return rounded[first][:, a - first : b - first, :]
+        gathered = {a0: rows(y[0], 0, b0), a1: rows(stage, 0, b1 - a1), a2: rows(y[0], TAIL_AT, TAIL_PITCH)}
+        rounded = keep.tile([P, S, PACK], BF16, name="rounded", align_bytes=64)
 
         def gather(first, js, a, b):
             for j in js:
@@ -103,13 +94,7 @@ def tile_moe_pre_lin_none_kernel(tc, xT, w_words, w_scales, gate, offs, pos1, po
         def interleave(a, b):
             first = max(f for f in gathered if f <= a)
             src = gathered[first][:, :, a - first : b - first].rearrange("p j (c s) -> p c j s", s=4)
-            if a == a3:
-                rounded[a] = stage[:, stride + a3 - a2 - 2 * (b - a) : stride + a3 - a2].bitcast(BF16).rearrange("p (s j) -> p s j", j=PACK)
-            dst = rounded_slots(a, b).rearrange("p (c s) j -> p c j s", s=4)
-            if a == a3:
-                nc.vector.tensor_copy(dst, src)
-            else:
-                nc.scalar.copy(dst, src)
+            nc.scalar.copy(rounded[:, a:b, :].rearrange("p (c s) j -> p c j s", s=4), src)
 
         codes = {}
         planes = {}
@@ -118,20 +103,19 @@ def tile_moe_pre_lin_none_kernel(tc, xT, w_words, w_scales, gate, offs, pos1, po
             a, b = SPANS[n]
             codes[n] = keep.tile([P, b - a], U32, name="codes%d" % n, align_bytes=64)
             planes[n] = keep.tile([P, b - a], U8, name="plane%d" % n, align_bytes=64)
-            src = rounded_slots(a, b)
+            src = rounded[:, a:b, :]
             nc.vector.quantize_mx(out=codes[n][:].bitcast(FP8X4), scales=planes[n][:], in_=src.rearrange("p s j -> p (s j)"))
 
-        acc = {}
+        def bank(tag):
+            return psum.tile([P, 512], F32, name=tag, tag=tag)
 
-        def multiply(b, h):
-            first, end = BANKS[b]
-            acc[b, h] = psum.tile([P, 512], F32, name="acc")
-            for e in range(first, end):
+        def multiply(acc, first, experts, h):
+            for e in experts:
                 n = [n for n, (lo, hi) in enumerate(SPANS) if lo <= e * C < hi][0]
                 w = [n for n, (lo, hi) in enumerate(W_CHUNKS) if lo <= e < hi][0]
                 cols = slice(e * C - SPANS[n][0], (e + 1) * C - SPANS[n][0])
                 nc.tensor.matmul_mx(
-                    out=acc[b, h][:, (e - first) * C : (e - first + 1) * C],
+                    out=acc[:, (e - first) * C : (e - first + 1) * C],
                     lhsT=w_codes[w][:, e - W_CHUNKS[w][0], 2 * P * h : 2 * P * (h + 1)].bitcast(FP4X4),
                     lhsT_scale=w_planes[w][:, e - W_CHUNKS[w][0], P * h : P * (h + 1)],
                     rhs=codes[n][:, cols].bitcast(FP8X4),
@@ -140,17 +124,11 @@ def tile_moe_pre_lin_none_kernel(tc, xT, w_words, w_scales, gate, offs, pos1, po
                     stop=True,
                 )
 
-        def empty(b, h, on_vector=False):
-            first, end = BANKS[b]
+        def empty(acc, first, end, h, on_vector=False):
             if on_vector:
-                nc.vector.tensor_copy(y[h][:, first * C : end * C], acc[b, h][:, : (end - first) * C])
+                nc.vector.tensor_copy(y[h][:, first * C : end * C], acc[:, : (end - first) * C])
             else:
-                nc.scalar.copy(y[h][:, first * C : end * C], acc[b, h][:, : (end - first) * C])
-
-        def bank(b):
-            for h in range(2):
-                multiply(b, h)
-                empty(b, h)
+                nc.scalar.copy(y[h][:, first * C : end * C], acc[:, : (end - first) * C])
 
         gather(a0, [0], *GATE_CHUNKS[0])
         gather(a0, [0], *GATE_CHUNKS[1])
@@ -160,24 +138,33 @@ def tile_moe_pre_lin_none_kernel(tc, xT, w_words, w_scales, gate, offs, pos1, po
         gather(a1, range(PACK), a1, b1)
         interleave(a1, b1)
         quantize(0)
-        bank(0)
-        gather(a2, [0, 1], a2, b3)
-        gather(a2, [2, 3], a2, b2)
+        for h in range(2):
+            acc = bank("early%d" % h)
+            multiply(acc, 0, range(4), h)
+            empty(acc, 0, 4, h)
+        gather(a2, [0, 2], a2, b3)
+        gather(a2, [1, 3], a2, b2)
         interleave(a2, b2)
+        late = {4: bank("late4"), 7: bank("late7"), 9: bank("late9"), 11: bank("late11")}
+        lone = bank("lone")
         quantize(1)
-        bank(1)
-        gather(a2, [2, 3], a3, b3)
-        quantize(2)
+        multiply(late[4], 4, [4], 0)
+        multiply(lone, 4, [4], 1)
+        gather(a2, [1, 3], a3, b3)
         interleave(a3, b3)
-        quantize(3)
-        quantize(4)
-        multiply(2, 0)
-        empty(2, 0)
-        multiply(2, 1)
-        empty(2, 1, True)
-        for b, h in ((4, 0), (5, 0), (3, 1)):
-            multiply(b, h)
-            empty(b, h)
+        for e in range(5, E):
+            quantize(e - 3)
+            first = max(f for f in late if f <= e)
+            multiply(late[first], first, [e], 0)
+        empty(late[4], 4, 7, 0)
+        empty(lone, 4, 5, 1)
+        empty(late[7], 7, 9, 0, True)
+        empty(late[9], 9, 11, 0, True)
+        empty(late[11], 11, 12, 0)
+        for tag, first, end in (("late4", 5, 8), ("late7", 8, 10), ("late9", 10, 12)):
+            acc = bank(tag)
+            multiply(acc, first, range(first, end), 1)
+            empty(acc, first, end, 1)
 
         sums = [[keep.tile([P, T], F32, name="sum%d_%d" % (h, r)) for r in range(3)] for h in range(2)]
 

@@ -25,7 +25,7 @@ WINDOW = 784
 GATE_CHUNKS = [(0, 256), (256, 768), (768, 1536)]
 W_CHUNKS = [(0, 4), (4, 12)]
 TOKEN_CUT = 384
-SPANS = [(0, 512)] + [(e * C, (e + 1) * C) for e in range(4, E)]
+SPANS = [(0, 512), (512, 640), (640, 896), (896, 1152), (1152, 1408), (1408, 1536)]
 TAIL_AT, TAIL_PITCH = 768, 384
 
 
@@ -44,6 +44,9 @@ def tile_moe_pre_lin_none_kernel(tc, xT, w_words, w_scales, gate, offs, pos1, po
         w_planes = [keep.tile([P, b - a, N], U8, name="w_plane%d" % a, align_bytes=64) for a, b in W_CHUNKS]
         y = [keep.tile([P, 2 * S], F32, name="y0", align_bytes=64), keep.tile([P, S], F32, name="y1")]
 
+        sums = [[keep.tile([P, T], F32, name="sum%d_%d" % (h, r)) for r in range(3)] for h in range(2)]
+        ones = sums[0][1][:, 0:1]
+
         x_hbm = xT.rearrange("(p j) t -> p j t", j=PACK)
         gate_hbm = gate.rearrange("(p j) s -> p j s", j=PACK)
         words_hbm = w_words.rearrange("e a p b -> p (e a) b")
@@ -61,6 +64,7 @@ def tile_moe_pre_lin_none_kernel(tc, xT, w_words, w_scales, gate, offs, pos1, po
 
         for plane in w_planes:
             nc.vector.memset(plane[:].bitcast(I32), 0)
+        nc.vector.memset(ones, 1.0)
         nc.sync.dma_start(x_rows[0][:, :T], x_hbm[:, 0, :])
         nc.sync.dma_start(slot_list[:], offs)
         load_gate(0)
@@ -150,23 +154,39 @@ def tile_moe_pre_lin_none_kernel(tc, xT, w_words, w_scales, gate, offs, pos1, po
         quantize(1)
         multiply(late[4], 4, [4], 0)
         multiply(lone, 4, [4], 1)
+        warm = bank("early1")
+        for width in (512, 256):
+            nc.tensor.matmul_mx(
+                out=warm[:, :width],
+                lhsT=w_codes[0][:, 0, : 2 * P].bitcast(FP4X4),
+                lhsT_scale=w_planes[0][:, 0, :P],
+                rhs=codes[0][:, :width].bitcast(FP8X4),
+                rhs_scale=planes[0][:, :width],
+                start=True,
+                stop=True,
+            )
         gather(a2, [1, 3], a3, b3)
         interleave(a3, b3)
-        for e in range(5, E):
-            quantize(e - 3)
-            first = max(f for f in late if f <= e)
-            multiply(late[first], first, [e], 0)
+        for n in range(2, len(SPANS)):
+            quantize(n)
+            experts = range(SPANS[n][0] // C, SPANS[n][1] // C)
+            first = max(f for f in late if f <= experts[0])
+            multiply(late[first], first, experts, 0)
+            if n == 2:
+                multiply(lone, 4, experts, 1)
         empty(late[4], 4, 7, 0)
-        empty(lone, 4, 5, 1)
+        empty(lone, 4, 7, 1)
         empty(late[7], 7, 9, 0, True)
         empty(late[9], 9, 11, 0, True)
         empty(late[11], 11, 12, 0)
-        for tag, first, end in (("late4", 5, 8), ("late7", 8, 10), ("late9", 10, 12)):
+        for tag, first, end in (("late4", 7, 10), ("late7", 10, 12)):
             acc = bank(tag)
             multiply(acc, first, range(first, end), 1)
-            empty(acc, first, end, 1)
+            if end < E:
+                empty(acc, first, end, 1)
+            else:
+                nc.scalar.activation(y[1][:, first * C :], acc[:, : (end - first) * C], mybir.ActivationFunctionType.Copy, scale=ones)
 
-        sums = [[keep.tile([P, T], F32, name="sum%d_%d" % (h, r)) for r in range(3)] for h in range(2)]
 
         def fetch(h, r, a, b):
             picked = y[h][:].indirect(back_lists[r][:, a // 16 : b // 16])

@@ -146,15 +146,7 @@ def tile_moe_pre_lin_none_kernel(tc, xT, w_words, w_scales, gate, offs, pos1, po
             acc = bank("early%d" % h)
             multiply(acc, 0, range(4), h)
             empty(acc, 0, 4, h)
-        gather(a2, [0, 2], a2, b3)
-        gather(a2, [1, 3], a2, b2)
-        interleave(a2, b2)
-        late = {4: bank("late4"), 7: bank("late7"), 9: bank("late9"), 11: bank("late11")}
-        lone = bank("lone")
-        quantize(1)
-        multiply(late[4], 4, [4], 0)
-        multiply(lone, 4, [4], 1)
-        warm = bank("early1")
+        warm = bank("early0")
         for width in (512, 256):
             nc.tensor.matmul_mx(
                 out=warm[:, :width],
@@ -165,6 +157,14 @@ def tile_moe_pre_lin_none_kernel(tc, xT, w_words, w_scales, gate, offs, pos1, po
                 start=True,
                 stop=True,
             )
+        gather(a2, [0, 2], a2, b3)
+        gather(a2, [1, 3], a2, b2)
+        interleave(a2, b2)
+        late = {4: bank("early0"), 7: bank("late7"), 9: bank("late9"), 11: bank("late11")}
+        lone = bank("early1")
+        quantize(1)
+        multiply(late[4], 4, [4], 0)
+        multiply(lone, 4, [4], 1)
         gather(a2, [1, 3], a3, b3)
         interleave(a3, b3)
         for n in range(2, len(SPANS)):
@@ -179,7 +179,7 @@ def tile_moe_pre_lin_none_kernel(tc, xT, w_words, w_scales, gate, offs, pos1, po
         empty(late[7], 7, 9, 0, True)
         empty(late[9], 9, 11, 0, True)
         empty(late[11], 11, 12, 0)
-        for tag, first, end in (("late4", 7, 10), ("late7", 10, 12)):
+        for tag, first, end in (("early0", 7, 10), ("late7", 10, 12)):
             acc = bank(tag)
             multiply(acc, first, range(first, end), 1)
             if end < E:

@@ -19,14 +19,14 @@ FP8X4 = mybir.dt.float8_e4m3fn_x4
 FP4X4 = mybir.dt.float4_e2m1fn_x4
 MULT = mybir.AluOpType.mult
 ADD = mybir.AluOpType.add
+COPY = mybir.ActivationFunctionType.Copy
 
-PIECES = [(0, 768), (768, 1216), (1216, 1408), (1408, 1536)]
-WINDOW = 784
-GATE_CHUNKS = [(0, 256), (256, 768), (768, 1536)]
-W_CHUNKS = [(0, 4), (4, 12)]
-TOKEN_CUT = 384
-SPANS = [(0, 512), (512, 640), (640, 896), (896, 1152), (1152, 1408), (1408, 1536)]
-TAIL_AT, TAIL_PITCH = 768, 384
+OWN = 480
+PIECES = [(OWN, 1088), (1088, 1408), (1408, S)]
+WINDOW = 640
+GATE_CHUNKS = [(0, 128), (128, OWN), (OWN, 1088), (1088, S)]
+SPANS = [(0, 384), (384, 896), (896, 1024), (1024, 1280), (1280, 1408), (1408, S)]
+RUN = 2
 
 
 def tile_moe_pre_lin_none_kernel(tc, xT, w_words, w_scales, gate, offs, pos1, pos2, pos3, out):
@@ -40,12 +40,10 @@ def tile_moe_pre_lin_none_kernel(tc, xT, w_words, w_scales, gate, offs, pos1, po
         back_lists = [lists.tile([P, T // 16], U16, name="back_list%d" % r) for r in range(3)]
         x_rows = [keep.tile([P, WINDOW], F32, name="x_row%d" % j) for j in range(PACK)]
         gates = keep.tile([P, S], F32, name="gates")
-        w_codes = [keep.tile([P, b - a, 2 * N], U8, name="w_codes%d" % a, align_bytes=64) for a, b in W_CHUNKS]
-        w_planes = [keep.tile([P, b - a, N], U8, name="w_plane%d" % a, align_bytes=64) for a, b in W_CHUNKS]
-        y = [keep.tile([P, 2 * S], F32, name="y0", align_bytes=64), keep.tile([P, S], F32, name="y1")]
-
-        sums = [[keep.tile([P, T], F32, name="sum%d_%d" % (h, r)) for r in range(3)] for h in range(2)]
-        ones = sums[0][1][:, 0:1]
+        w_codes = keep.tile([P, E, 2 * N], U8, name="w_codes", align_bytes=64)
+        w_plane = keep.tile([P, E, N], U8, name="w_plane", align_bytes=64)
+        y = [keep.tile([P, S], F32, name="y%d" % h) for h in range(2)]
+        sums = [[keep.tile([P, T], F32, name="sum%d_%d" % (h, r)) for r in range(4)] for h in range(2)]
 
         x_hbm = xT.rearrange("(p j) t -> p j t", j=PACK)
         gate_hbm = gate.rearrange("(p j) s -> p j s", j=PACK)
@@ -56,15 +54,8 @@ def tile_moe_pre_lin_none_kernel(tc, xT, w_words, w_scales, gate, offs, pos1, po
             a, b = GATE_CHUNKS[i]
             nc.sync.dma_start(gates[:, a:b], gate_hbm[:, 0, a:b])
 
-        def load_words(i):
-            a, b = W_CHUNKS[i]
-            for q in range(4):
-                nc.sync.dma_start(w_planes[i][32 * q : 32 * q + 4, :, :].bitcast(I32), scales_hbm[4 * q : 4 * q + 4, a:b, :].bitcast(I32))
-            nc.sync.dma_start(w_codes[i][:].bitcast(I32), words_hbm[:, a:b, :].bitcast(I32))
-
-        for plane in w_planes:
-            nc.vector.memset(plane[:].bitcast(I32), 0)
-        nc.vector.memset(ones, 1.0)
+        nc.vector.memset(w_plane[:, : E // 2, :].bitcast(U32), 0)
+        nc.scalar.copy(w_plane[:, E // 2 :, :].bitcast(U32), w_plane[:, : E // 2, :].bitcast(U32))
         nc.sync.dma_start(x_rows[0][:, :T], x_hbm[:, 0, :])
         nc.sync.dma_start(slot_list[:], offs)
         load_gate(0)
@@ -72,33 +63,31 @@ def tile_moe_pre_lin_none_kernel(tc, xT, w_words, w_scales, gate, offs, pos1, po
         for j in range(1, PACK):
             nc.sync.dma_start(x_rows[j][:, :T], x_hbm[:, j, :])
         load_gate(2)
-        load_words(0)
-        load_words(1)
+        for q in range(4):
+            nc.sync.dma_start(w_plane[32 * q : 32 * q + 4, :, :].bitcast(I32), scales_hbm[4 * q : 4 * q + 4, :, :].bitcast(I32))
+        nc.sync.dma_start(w_codes[:].bitcast(I32), words_hbm.bitcast(I32))
+        load_gate(3)
         for tile, pos in zip(back_lists, (pos1, pos2, pos3)):
             nc.sync.dma_start(tile[:], pos)
 
-        (a0, b0), (a1, b1), (a2, b2), (a3, b3) = PIECES
-        stage = keep.tile([P, PACK * (b1 - a1)], F32, name="stage", align_bytes=64)
-
-        def rows(tile, start, slots):
-            return tile[:, start : start + PACK * slots].rearrange("p (j s) -> p j s", j=PACK)
-
-        gathered = {a0: rows(y[0], 0, b0), a1: rows(stage, 0, b1 - a1), a2: rows(y[0], TAIL_AT, TAIL_PITCH)}
+        (a1, b1), (a2, b2), (a3, b3) = PIECES
+        stages = [keep.tile([P, PACK, width], F32, name="stage%d" % width) for width in (OWN, b1 - a1)]
+        gathered = {0: stages[0], a1: stages[1], a2: stages[0], a3: stages[1]}
         rounded = keep.tile([P, S, PACK], BF16, name="rounded", align_bytes=64)
 
-        def gather(first, js, a, b):
-            for j in js:
-                nc.vector.tensor_tensor(
-                    gathered[first][:, j, a - first : b - first],
-                    x_rows[j][:].indirect(slot_list[:, a // 16 : b // 16]),
-                    gates[:, a:b],
-                    MULT,
-                )
+        def window(j, a, b):
+            return x_rows[j][:].indirect(slot_list[:, a // 16 : b // 16])
 
-        def interleave(a, b):
+        def staged(a, b):
             first = max(f for f in gathered if f <= a)
-            src = gathered[first][:, :, a - first : b - first].rearrange("p j (c s) -> p c j s", s=4)
-            nc.scalar.copy(rounded[:, a:b, :].rearrange("p (c s) j -> p c j s", s=4), src)
+            return gathered[first][:, :, a - first : b - first].rearrange("p j (c s) -> p c j s", s=RUN)
+
+        def woven(a, b):
+            return rounded[:, a:b, :].rearrange("p (c s) j -> p c j s", s=RUN)
+
+        def weigh(a, b):
+            weights = gates[:, a:b].rearrange("p (c s) -> p c s", s=RUN).unsqueeze(2).to_broadcast([P, (b - a) // RUN, PACK, RUN])
+            nc.vector.tensor_tensor(woven(a, b), staged(a, b), weights, MULT)
 
         codes = {}
         planes = {}
@@ -107,99 +96,82 @@ def tile_moe_pre_lin_none_kernel(tc, xT, w_words, w_scales, gate, offs, pos1, po
             a, b = SPANS[n]
             codes[n] = keep.tile([P, b - a], U32, name="codes%d" % n, align_bytes=64)
             planes[n] = keep.tile([P, b - a], U8, name="plane%d" % n, align_bytes=64)
-            src = rounded[:, a:b, :]
-            nc.vector.quantize_mx(out=codes[n][:].bitcast(FP8X4), scales=planes[n][:], in_=src.rearrange("p s j -> p (s j)"))
+            nc.vector.quantize_mx(out=codes[n][:].bitcast(FP8X4), scales=planes[n][:], in_=rounded[:, a:b, :].rearrange("p s j -> p (s j)"))
 
-        def bank(tag):
-            return psum.tile([P, 512], F32, name=tag, tag=tag)
+        BANKS = [[(0, 4), (4, 8), (8, 11), (11, 12)], [(0, 4), (4, 8), (8, 12)]]
+        banks = [[psum.tile([P, 512], F32, name="bank%d_%d" % (h, a)) for a, b in BANKS[h]] for h in range(2)]
 
-        def multiply(acc, first, experts, h):
-            for e in experts:
-                n = [n for n, (lo, hi) in enumerate(SPANS) if lo <= e * C < hi][0]
-                w = [n for n, (lo, hi) in enumerate(W_CHUNKS) if lo <= e < hi][0]
+        def multiply(n, h):
+            for e in range(SPANS[n][0] // C, SPANS[n][1] // C):
+                i = [i for i, (lo, hi) in enumerate(BANKS[h]) if lo <= e < hi][0]
+                place = e - BANKS[h][i][0]
                 cols = slice(e * C - SPANS[n][0], (e + 1) * C - SPANS[n][0])
                 nc.tensor.matmul_mx(
-                    out=acc[:, (e - first) * C : (e - first + 1) * C],
-                    lhsT=w_codes[w][:, e - W_CHUNKS[w][0], 2 * P * h : 2 * P * (h + 1)].bitcast(FP4X4),
-                    lhsT_scale=w_planes[w][:, e - W_CHUNKS[w][0], P * h : P * (h + 1)],
+                    out=banks[h][i][:, place * C : (place + 1) * C],
+                    lhsT=w_codes[:, e, 2 * P * h : 2 * P * (h + 1)].bitcast(FP4X4),
+                    lhsT_scale=w_plane[:, e, P * h : P * (h + 1)],
                     rhs=codes[n][:, cols].bitcast(FP8X4),
                     rhs_scale=planes[n][:, cols],
                     start=True,
                     stop=True,
                 )
 
-        def empty(acc, first, end, h, on_vector=False):
-            if on_vector:
-                nc.vector.tensor_copy(y[h][:, first * C : end * C], acc[:, : (end - first) * C])
-            else:
-                nc.scalar.copy(y[h][:, first * C : end * C], acc[:, : (end - first) * C])
+        def empty(copy, h, i):
+            first, end = BANKS[h][i]
+            copy(y[h][:, first * C : end * C], banks[h][i][:, : (end - first) * C])
 
-        gather(a0, [0], *GATE_CHUNKS[0])
-        gather(a0, [0], *GATE_CHUNKS[1])
-        gather(a0, [1, 2, 3], a0, b0)
-        interleave(a0, 512)
-        interleave(512, b0)
-        gather(a1, range(PACK), a1, b1)
-        interleave(a1, b1)
+        def gather(a, b):
+            for j in range(PACK):
+                nc.scalar.activation(gathered[a][:, j, : b - a], window(j, a, b), COPY)
+
+        gather(a1, b1)
+        for j, (a, b) in [(0, GATE_CHUNKS[0]), (0, GATE_CHUNKS[1]), (1, (0, OWN)), (2, (0, OWN)), (3, (0, OWN))]:
+            nc.vector.tensor_tensor(gathered[0][:, j, a:b], window(j, a, b), gates[:, a:b], MULT)
+        nc.vector.tensor_copy(woven(0, OWN), staged(0, OWN))
+        gather(a2, b2)
         quantize(0)
-        for h in range(2):
-            acc = bank("early%d" % h)
-            multiply(acc, 0, range(4), h)
-            empty(acc, 0, 4, h)
-        warm = bank("early0")
-        for width in (512, 256):
-            nc.tensor.matmul_mx(
-                out=warm[:, :width],
-                lhsT=w_codes[0][:, 0, : 2 * P].bitcast(FP4X4),
-                lhsT_scale=w_planes[0][:, 0, :P],
-                rhs=codes[0][:, :width].bitcast(FP8X4),
-                rhs_scale=planes[0][:, :width],
-                start=True,
-                stop=True,
-            )
-        gather(a2, [0, 2], a2, b3)
-        gather(a2, [1, 3], a2, b2)
-        interleave(a2, b2)
-        late = {4: bank("early0"), 7: bank("late7"), 9: bank("late9"), 11: bank("late11")}
-        lone = bank("early1")
+        weigh(a1, 896)
+        weigh(896, b1)
+        gather(a3, b3)
         quantize(1)
-        multiply(late[4], 4, [4], 0)
-        multiply(lone, 4, [4], 1)
-        gather(a2, [1, 3], a3, b3)
-        interleave(a3, b3)
-        for n in range(2, len(SPANS)):
-            quantize(n)
-            experts = range(SPANS[n][0] // C, SPANS[n][1] // C)
-            first = max(f for f in late if f <= experts[0])
-            multiply(late[first], first, experts, 0)
-            if n == 2:
-                multiply(lone, 4, experts, 1)
-        empty(late[4], 4, 7, 0)
-        empty(lone, 4, 7, 1)
-        empty(late[7], 7, 9, 0, True)
-        empty(late[9], 9, 11, 0, True)
-        empty(late[11], 11, 12, 0)
-        for tag, first, end in (("early0", 7, 10), ("late7", 10, 12)):
-            acc = bank(tag)
-            multiply(acc, first, range(first, end), 1)
-            if end < E:
-                empty(acc, first, end, 1)
-            else:
-                nc.scalar.activation(y[1][:, first * C :], acc[:, : (end - first) * C], mybir.ActivationFunctionType.Copy, scale=ones)
+        quantize(2)
+        weigh(a2, 1280)
+        weigh(1280, b2)
+        quantize(3)
+        weigh(a3, b3)
+        quantize(4)
+        quantize(5)
+        for n in range(4):
+            multiply(n, 0)
+            multiply(n, 1)
+        for h in range(2):
+            multiply(4, h)
+            multiply(5, h)
+        for i in range(4):
+            empty(nc.scalar.copy, 0, i)
+        for i in range(3):
+            empty(nc.vector.tensor_copy, 1, i)
 
+        def picked(h, r, a, b):
+            return y[h][:].indirect(back_lists[r][:, a // 16 : b // 16])
 
         def fetch(h, r, a, b):
-            picked = y[h][:].indirect(back_lists[r][:, a // 16 : b // 16])
-            if r == 0:
-                nc.vector.tensor_copy(sums[h][0][:, a:b], picked)
-            else:
-                nc.vector.tensor_tensor(sums[h][r][:, a:b], picked, sums[h][r - 1][:, a:b], ADD)
+            nc.scalar.activation(sums[h][r][:, a:b], picked(h, r, a, b), COPY)
 
-        for r in range(2):
-            for h in range(2):
-                fetch(h, r, 0, T)
-        fetch(0, 2, 0, T)
+        def fetch_add(h, r, onto, a, b):
+            nc.vector.tensor_tensor(sums[h][r][:, a:b], picked(h, r, a, b), sums[h][onto][:, a:b], ADD)
+
+        H = T // 2
+        fetch(0, 0, 0, H)
+        fetch(0, 0, H, T)
+        fetch(1, 0, 0, T)
+        fetch(1, 1, 0, T)
+        fetch_add(0, 1, 0, 0, H)
+        fetch_add(0, 1, 0, H, T)
+        fetch_add(0, 2, 1, 0, H)
+        fetch_add(0, 2, 1, H, T)
         nc.sync.dma_start(out[0:P, :], sums[0][2][:])
-        for a, b in [(0, TOKEN_CUT), (TOKEN_CUT, T)]:
-            fetch(1, 2, a, b)
-            nc.sync.dma_start(out[P : 2 * P, a:b], sums[1][2][:, a:b])
+        fetch_add(1, 2, 0, 0, T)
+        for a, b in [(0, 384), (384, T)]:
+            nc.vector.tensor_tensor(sums[1][3][:, a:b], sums[1][2][:, a:b], sums[1][1][:, a:b], ADD)
+            nc.sync.dma_start(out[P : 2 * P, a:b], sums[1][3][:, a:b])

@@ -22,10 +22,11 @@ ADD = mybir.AluOpType.add
 COPY = mybir.ActivationFunctionType.Copy
 
 OWN = 480
-PIECES = [(OWN, 1088), (1088, 1408), (1408, S)]
-WINDOW = 640
-GATE_CHUNKS = [(0, 128), (128, OWN), (OWN, 1088), (1088, S)]
-SPANS = [(0, 384), (384, 896), (896, 1024), (1024, 1280), (1280, 1408), (1408, S)]
+PIECES = [(OWN, 1056), (1056, 1408), (1408, S)]
+WINDOW = 592
+GATE_CHUNKS = [(0, 128), (128, OWN), (OWN, 1056), (1056, S)]
+SPANS = [(0, 384), (384, 896), (896, 1280), (1280, 1408), (1408, S)]
+OWN_CUT = 256
 RUN = 2
 
 
@@ -39,7 +40,18 @@ def tile_moe_pre_lin_none_kernel(tc, xT, w_words, w_scales, gate, offs, pos1, po
         slot_list = lists.tile([P, S // 16], U16, name="slot_list")
         back_lists = [lists.tile([P, T // 16], U16, name="back_list%d" % r) for r in range(3)]
         x_rows = [keep.tile([P, WINDOW], F32, name="x_row%d" % j) for j in range(PACK)]
-        gates = keep.tile([P, S], F32, name="gates")
+        (a1, b1), (a2, b2), (a3, b3) = PIECES
+        stage_own = keep.tile([P, PACK, OWN], F32, name="stage_own")
+        stage1 = keep.tile([P, PACK, b1 - a1], F32, name="stage1")
+        stage2 = keep.tile([P, PACK * (b2 - a2)], F32, name="stage2")
+        late_gates = keep.tile([P, S - OWN], F32, name="late_gates")
+        own_at = (3 * (b2 - a2) - OWN) // 2
+
+        def gates(a, b):
+            if a < OWN:
+                return stage2[:, own_at + a : own_at + b]
+            return late_gates[:, a - OWN : b - OWN]
+
         w_codes = keep.tile([P, E, 2 * N], U8, name="w_codes", align_bytes=64)
         w_plane = keep.tile([P, E, N], U8, name="w_plane", align_bytes=64)
         y = [keep.tile([P, S], F32, name="y%d" % h) for h in range(2)]
@@ -52,7 +64,7 @@ def tile_moe_pre_lin_none_kernel(tc, xT, w_words, w_scales, gate, offs, pos1, po
 
         def load_gate(i):
             a, b = GATE_CHUNKS[i]
-            nc.sync.dma_start(gates[:, a:b], gate_hbm[:, 0, a:b])
+            nc.sync.dma_start(gates(a, b), gate_hbm[:, 0, a:b])
 
         nc.vector.memset(w_plane[:, : E // 2, :].bitcast(U32), 0)
         nc.scalar.copy(w_plane[:, E // 2 :, :].bitcast(U32), w_plane[:, : E // 2, :].bitcast(U32))
@@ -70,9 +82,7 @@ def tile_moe_pre_lin_none_kernel(tc, xT, w_words, w_scales, gate, offs, pos1, po
         for tile, pos in zip(back_lists, (pos1, pos2, pos3)):
             nc.sync.dma_start(tile[:], pos)
 
-        (a1, b1), (a2, b2), (a3, b3) = PIECES
-        stages = [keep.tile([P, PACK, width], F32, name="stage%d" % width) for width in (OWN, b1 - a1)]
-        gathered = {0: stages[0], a1: stages[1], a2: stages[0], a3: stages[1]}
+        gathered = {0: stage_own, a1: stage1, a2: stage2[:].rearrange("p (j s) -> p j s", j=PACK), a3: stage_own}
         rounded = keep.tile([P, S, PACK], BF16, name="rounded", align_bytes=64)
 
         def window(j, a, b):
@@ -86,7 +96,7 @@ def tile_moe_pre_lin_none_kernel(tc, xT, w_words, w_scales, gate, offs, pos1, po
             return rounded[:, a:b, :].rearrange("p (c s) j -> p c j s", s=RUN)
 
         def weigh(a, b):
-            weights = gates[:, a:b].rearrange("p (c s) -> p c s", s=RUN).unsqueeze(2).to_broadcast([P, (b - a) // RUN, PACK, RUN])
+            weights = gates(a, b).rearrange("p (c s) -> p c s", s=RUN).unsqueeze(2).to_broadcast([P, (b - a) // RUN, PACK, RUN])
             nc.vector.tensor_tensor(woven(a, b), staged(a, b), weights, MULT)
 
         codes = {}
@@ -98,8 +108,14 @@ def tile_moe_pre_lin_none_kernel(tc, xT, w_words, w_scales, gate, offs, pos1, po
             planes[n] = keep.tile([P, b - a], U8, name="plane%d" % n, align_bytes=64)
             nc.vector.quantize_mx(out=codes[n][:].bitcast(FP8X4), scales=planes[n][:], in_=rounded[:, a:b, :].rearrange("p s j -> p (s j)"))
 
-        BANKS = [[(0, 4), (4, 8), (8, 11), (11, 12)], [(0, 4), (4, 8), (8, 12)]]
-        banks = [[psum.tile([P, 512], F32, name="bank%d_%d" % (h, a)) for a, b in BANKS[h]] for h in range(2)]
+        BANKS = [[(0, 3), (3, 7), (7, 10), (10, 11), (11, 12)], [(0, 3), (3, 7), (7, 10), (10, 12)]]
+        banks = {}
+
+        def bank(h, i):
+            if (h, i) not in banks:
+                tag = "bank0_0" if (h, i) == (1, 3) else "bank%d_%d" % (h, i)
+                banks[h, i] = psum.tile([P, 512], F32, name=tag, tag=tag)
+            return banks[h, i]
 
         def multiply(n, h):
             for e in range(SPANS[n][0] // C, SPANS[n][1] // C):
@@ -107,7 +123,7 @@ def tile_moe_pre_lin_none_kernel(tc, xT, w_words, w_scales, gate, offs, pos1, po
                 place = e - BANKS[h][i][0]
                 cols = slice(e * C - SPANS[n][0], (e + 1) * C - SPANS[n][0])
                 nc.tensor.matmul_mx(
-                    out=banks[h][i][:, place * C : (place + 1) * C],
+                    out=bank(h, i)[:, place * C : (place + 1) * C],
                     lhsT=w_codes[:, e, 2 * P * h : 2 * P * (h + 1)].bitcast(FP4X4),
                     lhsT_scale=w_plane[:, e, P * h : P * (h + 1)],
                     rhs=codes[n][:, cols].bitcast(FP8X4),
@@ -118,38 +134,40 @@ def tile_moe_pre_lin_none_kernel(tc, xT, w_words, w_scales, gate, offs, pos1, po
 
         def empty(copy, h, i):
             first, end = BANKS[h][i]
-            copy(y[h][:, first * C : end * C], banks[h][i][:, : (end - first) * C])
+            copy(y[h][:, first * C : end * C], bank(h, i)[:, : (end - first) * C])
 
         def gather(a, b):
             for j in range(PACK):
                 nc.scalar.activation(gathered[a][:, j, : b - a], window(j, a, b), COPY)
 
         gather(a1, b1)
-        for j, (a, b) in [(0, GATE_CHUNKS[0]), (0, GATE_CHUNKS[1]), (1, (0, OWN)), (2, (0, OWN)), (3, (0, OWN))]:
-            nc.vector.tensor_tensor(gathered[0][:, j, a:b], window(j, a, b), gates[:, a:b], MULT)
-        nc.vector.tensor_copy(woven(0, OWN), staged(0, OWN))
+        for j, (a, b) in [(0, GATE_CHUNKS[0]), (0, GATE_CHUNKS[1]), (1, (0, OWN)), (2, (0, OWN)), (3, (0, OWN_CUT)), (3, (OWN_CUT, OWN))]:
+            nc.vector.tensor_tensor(gathered[0][:, j, a:b], window(j, a, b), gates(a, b), MULT)
         gather(a2, b2)
-        quantize(0)
-        weigh(a1, 896)
-        weigh(896, b1)
+        for a, b in [(0, OWN_CUT), (OWN_CUT, OWN)]:
+            nc.vector.tensor_copy(woven(a, b), staged(a, b))
         gather(a3, b3)
+        weigh(a1, 896)
+        quantize(0)
+        weigh(896, b1)
         quantize(1)
-        quantize(2)
         weigh(a2, 1280)
         weigh(1280, b2)
-        quantize(3)
+        quantize(2)
         weigh(a3, b3)
+        quantize(3)
         quantize(4)
-        quantize(5)
-        for n in range(4):
+        for n in range(3):
             multiply(n, 0)
             multiply(n, 1)
-        for h in range(2):
-            multiply(4, h)
-            multiply(5, h)
-        for i in range(4):
-            empty(nc.scalar.copy, 0, i)
-        for i in range(3):
+        multiply(3, 0)
+        multiply(4, 0)
+        for h, i in [(0, 0), (0, 1), (1, 0), (0, 2), (0, 3), (0, 4)]:
+            empty(nc.scalar.copy, h, i)
+        multiply(3, 1)
+        multiply(4, 1)
+        empty(nc.scalar.copy, 1, 3)
+        for i in (1, 2):
             empty(nc.vector.tensor_copy, 1, i)
 
         def picked(h, r, a, b):
@@ -159,19 +177,20 @@ def tile_moe_pre_lin_none_kernel(tc, xT, w_words, w_scales, gate, offs, pos1, po
             nc.scalar.activation(sums[h][r][:, a:b], picked(h, r, a, b), COPY)
 
         def fetch_add(h, r, onto, a, b):
-            nc.vector.tensor_tensor(sums[h][r][:, a:b], picked(h, r, a, b), sums[h][onto][:, a:b], ADD)
+            nc.vector.tensor_tensor(sums[h][r][:, a:b], picked(h, min(r, 2), a, b), sums[h][onto][:, a:b], ADD)
 
-        H = T // 2
-        fetch(0, 0, 0, H)
-        fetch(0, 0, H, T)
+        A = 192
+        nc.vector.tensor_copy(sums[0][0][:, :A], picked(0, 0, 0, A))
+        fetch(0, 0, A, T)
         fetch(1, 0, 0, T)
-        fetch(1, 1, 0, T)
-        fetch_add(0, 1, 0, 0, H)
-        fetch_add(0, 1, 0, H, T)
-        fetch_add(0, 2, 1, 0, H)
-        fetch_add(0, 2, 1, H, T)
-        nc.sync.dma_start(out[0:P, :], sums[0][2][:])
+        fetch(0, 1, A, T)
+        fetch(1, 1, 0, 384)
+        fetch(1, 1, 384, T)
+        fetch_add(0, 1, 0, 0, A)
+        fetch_add(0, 2, 0, A, T)
+        fetch_add(0, 3, 1, 0, A)
+        nc.sync.dma_start(out[0:P, :A], sums[0][3][:, :A])
         fetch_add(1, 2, 0, 0, T)
-        for a, b in [(0, 384), (384, T)]:
-            nc.vector.tensor_tensor(sums[1][3][:, a:b], sums[1][2][:, a:b], sums[1][1][:, a:b], ADD)
-            nc.sync.dma_start(out[P : 2 * P, a:b], sums[1][3][:, a:b])
+        for h, a, b in [(0, A, T), (1, 0, 384), (1, 384, T)]:
+            nc.vector.tensor_tensor(sums[h][3][:, a:b], sums[h][2][:, a:b], sums[h][1][:, a:b], ADD)
+            nc.sync.dma_start(out[h * P : (h + 1) * P, a:b], sums[h][3][:, a:b])

@@ -1,6 +1,7 @@
 from contextlib import ExitStack
 
 import concourse.mybir as mybir
+from concourse.masks import make_identity
 
 K, T, E, C, N = 512, 512, 12, 128, 256
 S = E * C
@@ -21,12 +22,11 @@ MULT = mybir.AluOpType.mult
 ADD = mybir.AluOpType.add
 COPY = mybir.ActivationFunctionType.Copy
 
-OWN = 480
-PIECES = [(OWN, 1056), (1056, 1408), (1408, S)]
-WINDOW = 592
-GATE_CHUNKS = [(0, 128), (128, OWN), (OWN, 1056), (1056, S)]
-SPANS = [(0, 384), (384, 896), (896, 1280), (1280, 1408), (1408, S)]
-OWN_CUT = 256
+OWN = 512
+PIECES = [(OWN, 1024), (1024, 1280), (1280, S)]
+WINDOW = 528
+GATE_CHUNKS = [(0, 128), (128, OWN)]
+SPANS = [(0, 512), (512, 1024), (1024, 1280), (1280, 1408), (1408, S)]
 RUN = 2
 
 
@@ -43,14 +43,18 @@ def tile_moe_pre_lin_none_kernel(tc, xT, w_words, w_scales, gate, offs, pos1, po
         (a1, b1), (a2, b2), (a3, b3) = PIECES
         stage_own = keep.tile([P, PACK, OWN], F32, name="stage_own")
         stage1 = keep.tile([P, PACK, b1 - a1], F32, name="stage1")
-        stage2 = keep.tile([P, PACK * (b2 - a2)], F32, name="stage2")
-        late_gates = keep.tile([P, S - OWN], F32, name="late_gates")
+        stage2 = keep.tile([P, PACK * (b2 - a2)], F32, name="stage2", tag="stage2", align_bytes=64)
+        stage3 = keep.tile([P, PACK * (b3 - a3)], F32, name="stage3")
         own_at = (3 * (b2 - a2) - OWN) // 2
+        first_columns = keep.tile([P, PACK * 8], F32, name="first_columns")
+        gate_columns = [first_columns[:, ::8], stage3[:, :: b3 - a3]]
+        identity = keep.tile([P, P], F32, name="identity")
 
         def gates(a, b):
-            if a < OWN:
-                return stage2[:, own_at + a : own_at + b]
-            return late_gates[:, a - OWN : b - OWN]
+            return stage2[:, own_at + a : own_at + b]
+
+        def bank(tag):
+            return psum.tile([P, 512], F32, name=tag, tag=tag)
 
         w_codes = keep.tile([P, E, 2 * N], U8, name="w_codes", align_bytes=64)
         w_plane = keep.tile([P, E, N], U8, name="w_plane", align_bytes=64)
@@ -59,6 +63,7 @@ def tile_moe_pre_lin_none_kernel(tc, xT, w_words, w_scales, gate, offs, pos1, po
 
         x_hbm = xT.rearrange("(p j) t -> p j t", j=PACK)
         gate_hbm = gate.rearrange("(p j) s -> p j s", j=PACK)
+        gate_blocks = gate[0, :].rearrange("(c n) -> n c", n=C)
         words_hbm = w_words.rearrange("e a p b -> p (e a) b")
         scales_hbm = w_scales.rearrange("e a q n -> q (e a) n")
 
@@ -74,16 +79,28 @@ def tile_moe_pre_lin_none_kernel(tc, xT, w_words, w_scales, gate, offs, pos1, po
         load_gate(1)
         for j in range(1, PACK):
             nc.sync.dma_start(x_rows[j][:, :T], x_hbm[:, j, :])
-        load_gate(2)
+        with nc.allow_non_contiguous_dma(reason="one gate value a partition"):
+            nc.sync.dma_start(gate_columns[0], gate_blocks[:, 4:8])
+            nc.sync.dma_start(gate_columns[1], gate_blocks[:, 8:12])
         for q in range(4):
             nc.sync.dma_start(w_plane[32 * q : 32 * q + 4, :, :].bitcast(I32), scales_hbm[4 * q : 4 * q + 4, :, :].bitcast(I32))
         nc.sync.dma_start(w_codes[:].bitcast(I32), words_hbm.bitcast(I32))
-        load_gate(3)
         for tile, pos in zip(back_lists, (pos1, pos2, pos3)):
             nc.sync.dma_start(tile[:], pos)
 
-        gathered = {0: stage_own, a1: stage1, a2: stage2[:].rearrange("p (j s) -> p j s", j=PACK), a3: stage_own}
-        rounded = keep.tile([P, S, PACK], BF16, name="rounded", align_bytes=64)
+        make_identity(nc, identity[:])
+        late_gates = [bank("g0"), bank("g1")]
+        for i in range(2):
+            for b in range(PACK):
+                nc.tensor.transpose(late_gates[i][:, b * C : (b + 1) * C], gate_columns[i][:, b : b + 1].to_broadcast([P, P]), identity[:])
+
+        gathered = {0: stage_own, a1: stage1}
+        for a, stage in ((a2, stage2), (a3, stage3)):
+            gathered[a] = stage[:].rearrange("p (j s) -> p j s", j=PACK)
+        rounded_tile = keep.tile([P, a3, PACK], BF16, name="rounded", align_bytes=64)
+
+        def rounded(a, b):
+            return rounded_tile[:, a % a3 : a % a3 + b - a, :]
 
         def window(j, a, b):
             return x_rows[j][:].indirect(slot_list[:, a // 16 : b // 16])
@@ -93,10 +110,10 @@ def tile_moe_pre_lin_none_kernel(tc, xT, w_words, w_scales, gate, offs, pos1, po
             return gathered[first][:, :, a - first : b - first].rearrange("p j (c s) -> p c j s", s=RUN)
 
         def woven(a, b):
-            return rounded[:, a:b, :].rearrange("p (c s) j -> p c j s", s=RUN)
+            return rounded(a, b).rearrange("p (c s) j -> p c j s", s=RUN)
 
         def weigh(a, b):
-            weights = gates(a, b).rearrange("p (c s) -> p c s", s=RUN).unsqueeze(2).to_broadcast([P, (b - a) // RUN, PACK, RUN])
+            weights = late_gates[(a - OWN) // 512][:, a % 512 : a % 512 + b - a].rearrange("p (c s) -> p c s", s=RUN).unsqueeze(2).to_broadcast([P, (b - a) // RUN, PACK, RUN])
             nc.vector.tensor_tensor(woven(a, b), staged(a, b), weights, MULT)
 
         codes = {}
@@ -104,17 +121,17 @@ def tile_moe_pre_lin_none_kernel(tc, xT, w_words, w_scales, gate, offs, pos1, po
 
         def quantize(n):
             a, b = SPANS[n]
-            codes[n] = keep.tile([P, b - a], U32, name="codes%d" % n, align_bytes=64)
+            codes[n] = keep.tile([P, b - a], U32, name="codes%d" % n, tag="stage2" if n == 0 else "codes%d" % n, align_bytes=64)
             planes[n] = keep.tile([P, b - a], U8, name="plane%d" % n, align_bytes=64)
-            nc.vector.quantize_mx(out=codes[n][:].bitcast(FP8X4), scales=planes[n][:], in_=rounded[:, a:b, :].rearrange("p s j -> p (s j)"))
+            nc.vector.quantize_mx(out=codes[n][:].bitcast(FP8X4), scales=planes[n][:], in_=rounded(a, b).rearrange("p s j -> p (s j)"))
 
-        BANKS = [[(0, 3), (3, 7), (7, 10), (10, 11), (11, 12)], [(0, 3), (3, 7), (7, 10), (10, 12)]]
+        BANKS = [[(0, 4), (4, 8), (8, 10), (10, 11), (11, 12)], [(0, 4), (4, 8), (8, 12)]]
+        TAGS = [["a", "c", "e", "f", "a"], ["b", "d", "g0"]]
         banks = {}
 
-        def bank(h, i):
+        def sums_bank(h, i):
             if (h, i) not in banks:
-                tag = "bank0_0" if (h, i) == (1, 3) else "bank%d_%d" % (h, i)
-                banks[h, i] = psum.tile([P, 512], F32, name=tag, tag=tag)
+                banks[h, i] = bank(TAGS[h][i])
             return banks[h, i]
 
         def multiply(n, h):
@@ -123,7 +140,7 @@ def tile_moe_pre_lin_none_kernel(tc, xT, w_words, w_scales, gate, offs, pos1, po
                 place = e - BANKS[h][i][0]
                 cols = slice(e * C - SPANS[n][0], (e + 1) * C - SPANS[n][0])
                 nc.tensor.matmul_mx(
-                    out=bank(h, i)[:, place * C : (place + 1) * C],
+                    out=sums_bank(h, i)[:, place * C : (place + 1) * C],
                     lhsT=w_codes[:, e, 2 * P * h : 2 * P * (h + 1)].bitcast(FP4X4),
                     lhsT_scale=w_plane[:, e, P * h : P * (h + 1)],
                     rhs=codes[n][:, cols].bitcast(FP8X4),
@@ -134,40 +151,42 @@ def tile_moe_pre_lin_none_kernel(tc, xT, w_words, w_scales, gate, offs, pos1, po
 
         def empty(copy, h, i):
             first, end = BANKS[h][i]
-            copy(y[h][:, first * C : end * C], bank(h, i)[:, : (end - first) * C])
+            copy(y[h][:, first * C : end * C], sums_bank(h, i)[:, : (end - first) * C])
 
         def gather(a, b):
             for j in range(PACK):
                 nc.scalar.activation(gathered[a][:, j, : b - a], window(j, a, b), COPY)
 
         gather(a1, b1)
-        for j, (a, b) in [(0, GATE_CHUNKS[0]), (0, GATE_CHUNKS[1]), (1, (0, OWN)), (2, (0, OWN)), (3, (0, OWN_CUT)), (3, (OWN_CUT, OWN))]:
+        for j, (a, b) in [(0, GATE_CHUNKS[0]), (0, GATE_CHUNKS[1]), (1, (0, OWN)), (2, (0, OWN)), (3, (0, OWN))]:
             nc.vector.tensor_tensor(gathered[0][:, j, a:b], window(j, a, b), gates(a, b), MULT)
         gather(a2, b2)
-        for a, b in [(0, OWN_CUT), (OWN_CUT, OWN)]:
-            nc.vector.tensor_copy(woven(a, b), staged(a, b))
         gather(a3, b3)
-        weigh(a1, 896)
-        quantize(0)
-        weigh(896, b1)
+        nc.gpsimd.tensor_scalar(rounded(0, OWN), stage_own[:].rearrange("p j s -> p s j"), 1.0, 0.0, MULT, ADD)
+        weigh(a1, b1)
+        weigh(a2, b2)
         quantize(1)
-        weigh(a2, 1280)
-        weigh(1280, b2)
+        quantize(0)
         quantize(2)
-        weigh(a3, b3)
+        weigh(a3, 1408)
+        weigh(1408, b3)
         quantize(3)
         quantize(4)
-        for n in range(3):
+        for n in (1, 0):
             multiply(n, 0)
-            multiply(n, 1)
+        for h, i in [(0, 1), (0, 0)]:
+            empty(nc.scalar.copy, h, i)
+        multiply(1, 1)
+        multiply(2, 0)
+        multiply(0, 1)
         multiply(3, 0)
         multiply(4, 0)
-        for h, i in [(0, 0), (0, 1), (1, 0), (0, 2), (0, 3), (0, 4)]:
-            empty(nc.scalar.copy, h, i)
-        multiply(3, 1)
-        multiply(4, 1)
-        empty(nc.scalar.copy, 1, 3)
-        for i in (1, 2):
+        for i in (2, 3, 4):
+            empty(nc.scalar.copy, 0, i)
+        for n in (2, 3, 4):
+            multiply(n, 1)
+        empty(nc.scalar.copy, 1, 2)
+        for i in (1, 0):
             empty(nc.vector.tensor_copy, 1, i)
 
         def picked(h, r, a, b):
@@ -191,6 +210,6 @@ def tile_moe_pre_lin_none_kernel(tc, xT, w_words, w_scales, gate, offs, pos1, po
         fetch_add(0, 3, 1, 0, A)
         nc.sync.dma_start(out[0:P, :A], sums[0][3][:, :A])
         fetch_add(1, 2, 0, 0, T)
-        for h, a, b in [(0, A, T), (1, 0, 384), (1, 384, T)]:
+        for h, a, b in [(0, A, T), (1, 0, 256), (1, 256, 384), (1, 384, T)]:
             nc.vector.tensor_tensor(sums[h][3][:, a:b], sums[h][2][:, a:b], sums[h][1][:, a:b], ADD)
             nc.sync.dma_start(out[h * P : (h + 1) * P, a:b], sums[h][3][:, a:b])

@@ -22,12 +22,12 @@ MULT = mybir.AluOpType.mult
 ADD = mybir.AluOpType.add
 COPY = mybir.ActivationFunctionType.Copy
 
-OWN = 512
-PIECES = [(OWN, 1024), (1024, 1280), (1280, S)]
+OWN = 256
+SPREAD_END = 1280
+PIECES = [(OWN, 576), (576, 960), (960, 1152), (1152, SPREAD_END)]
 WINDOW = 528
-GATE_CHUNKS = [(0, 128), (128, OWN)]
-SPANS = [(0, 512), (512, 1024), (1024, 1280), (1280, 1408), (1408, S)]
-RUN = 2
+SPANS = [(0, 512), (SPREAD_END, S), (512, 896), (896, 1152), (1152, SPREAD_END)]
+RUN = 4
 
 
 def tile_moe_pre_lin_none_kernel(tc, xT, w_words, w_scales, gate, offs, pos1, pos2, pos3, out):
@@ -40,18 +40,13 @@ def tile_moe_pre_lin_none_kernel(tc, xT, w_words, w_scales, gate, offs, pos1, po
         slot_list = lists.tile([P, S // 16], U16, name="slot_list")
         back_lists = [lists.tile([P, T // 16], U16, name="back_list%d" % r) for r in range(3)]
         x_rows = [keep.tile([P, WINDOW], F32, name="x_row%d" % j) for j in range(PACK)]
-        (a1, b1), (a2, b2), (a3, b3) = PIECES
-        stage_own = keep.tile([P, PACK, OWN], F32, name="stage_own")
-        stage1 = keep.tile([P, PACK, b1 - a1], F32, name="stage1")
-        stage2 = keep.tile([P, PACK * (b2 - a2)], F32, name="stage2", tag="stage2", align_bytes=64)
-        stage3 = keep.tile([P, PACK * (b3 - a3)], F32, name="stage3")
-        own_at = (3 * (b2 - a2) - OWN) // 2
-        first_columns = keep.tile([P, PACK * 8], F32, name="first_columns")
-        gate_columns = [first_columns[:, ::8], stage3[:, :: b3 - a3]]
+        (a1, b1), (a2, b2), (a3, b3), (a4, b4) = PIECES
+        first_gates = keep.tile([P, OWN], F32, name="first_gates", tag="second_piece")
+        last_gates = keep.tile([P, OWN], F32, name="last_gates", tag="fourth_piece")
+        gate_columns = keep.tile([P, 2, 2 * RUN], F32, name="gate_columns")
+        stage_own = keep.tile([P, PACK * OWN], F32, name="stage_own")
+        stage_shared = keep.tile([P, OWN + PACK * (b1 - a1)], F32, name="stage_shared")
         identity = keep.tile([P, P], F32, name="identity")
-
-        def gates(a, b):
-            return stage2[:, own_at + a : own_at + b]
 
         def bank(tag):
             return psum.tile([P, 512], F32, name=tag, tag=tag)
@@ -63,25 +58,19 @@ def tile_moe_pre_lin_none_kernel(tc, xT, w_words, w_scales, gate, offs, pos1, po
 
         x_hbm = xT.rearrange("(p j) t -> p j t", j=PACK)
         gate_hbm = gate.rearrange("(p j) s -> p j s", j=PACK)
-        gate_blocks = gate[0, :].rearrange("(c n) -> n c", n=C)
         words_hbm = w_words.rearrange("e a p b -> p (e a) b")
         scales_hbm = w_scales.rearrange("e a q n -> q (e a) n")
-
-        def load_gate(i):
-            a, b = GATE_CHUNKS[i]
-            nc.sync.dma_start(gates(a, b), gate_hbm[:, 0, a:b])
 
         nc.vector.memset(w_plane[:, : E // 2, :].bitcast(U32), 0)
         nc.scalar.copy(w_plane[:, E // 2 :, :].bitcast(U32), w_plane[:, : E // 2, :].bitcast(U32))
         nc.sync.dma_start(x_rows[0][:, :T], x_hbm[:, 0, :])
         nc.sync.dma_start(slot_list[:], offs)
-        load_gate(0)
-        load_gate(1)
-        for j in range(1, PACK):
+        nc.sync.dma_start(first_gates[:], gate_hbm[:, 0, :OWN])
+        for j in (1, 2):
             nc.sync.dma_start(x_rows[j][:, :T], x_hbm[:, j, :])
-        with nc.allow_non_contiguous_dma(reason="one gate value a partition"):
-            nc.sync.dma_start(gate_columns[0], gate_blocks[:, 4:8])
-            nc.sync.dma_start(gate_columns[1], gate_blocks[:, 8:12])
+        nc.sync.dma_start(gate_columns[:, :, :RUN], gate[0, OWN:SPREAD_END].rearrange("(g n b) -> n g b", g=2, b=RUN))
+        nc.sync.dma_start(x_rows[3][:, :T], x_hbm[:, 3, :])
+        nc.sync.dma_start(last_gates[:], gate_hbm[:, 0, SPREAD_END:])
         for q in range(4):
             nc.sync.dma_start(w_plane[32 * q : 32 * q + 4, :, :].bitcast(I32), scales_hbm[4 * q : 4 * q + 4, :, :].bitcast(I32))
         nc.sync.dma_start(w_codes[:].bitcast(I32), words_hbm.bitcast(I32))
@@ -89,58 +78,48 @@ def tile_moe_pre_lin_none_kernel(tc, xT, w_words, w_scales, gate, offs, pos1, po
             nc.sync.dma_start(tile[:], pos)
 
         make_identity(nc, identity[:])
-        late_gates = [bank("g0"), bank("g1")]
-        for i in range(2):
-            for b in range(PACK):
-                nc.tensor.transpose(late_gates[i][:, b * C : (b + 1) * C], gate_columns[i][:, b : b + 1].to_broadcast([P, P]), identity[:])
+        spread_gates = [bank("g0"), bank("g1")]
+        for g in range(2):
+            for b in range(RUN):
+                nc.tensor.transpose(spread_gates[g][:, b * P : (b + 1) * P], gate_columns[:, g, b : b + 1].to_broadcast([P, P]), identity[:])
 
-        gathered = {0: stage_own, a1: stage1}
-        for a, stage in ((a2, stage2), (a3, stage3)):
-            gathered[a] = stage[:].rearrange("p (j s) -> p j s", j=PACK)
-        rounded_tile = keep.tile([P, a3, PACK], BF16, name="rounded", align_bytes=64)
+        stages = {0: stage_own[:], a1: stage_shared[:, OWN:], SPREAD_END: stage_shared[:, : PACK * OWN], a3: stage_own[:, : PACK * (b3 - a3)]}
+        rounded_tile = keep.tile([P, 1024, PACK], BF16, name="rounded", align_bytes=64)
 
         def rounded(a, b):
-            return rounded_tile[:, a % a3 : a % a3 + b - a, :]
+            at = a + 192 if a < 512 else a - 512
+            return rounded_tile[:, at : at + b - a, :]
 
         def window(j, a, b):
             return x_rows[j][:].indirect(slot_list[:, a // 16 : b // 16])
 
         def staged(a, b):
-            first = max(f for f in gathered if f <= a)
-            return gathered[first][:, :, a - first : b - first].rearrange("p j (c s) -> p c j s", s=RUN)
-
-        def woven(a, b):
-            return rounded(a, b).rearrange("p (c s) j -> p c j s", s=RUN)
+            first = max(f for f in stages if f <= a)
+            return stages[first].rearrange("p (j s) -> p j s", j=PACK)[:, :, a - first : b - first]
 
         def weigh(a, b):
-            weights = late_gates[(a - OWN) // 512][:, a % 512 : a % 512 + b - a].rearrange("p (c s) -> p c s", s=RUN).unsqueeze(2).to_broadcast([P, (b - a) // RUN, PACK, RUN])
-            nc.vector.tensor_tensor(woven(a, b), staged(a, b), weights, MULT)
+            g, at = divmod(a - OWN, 512)
+            weights = spread_gates[g][:].rearrange("p (s c) -> p c s", s=RUN)[:, at // RUN : (at + b - a) // RUN, :].unsqueeze(2).to_broadcast([P, (b - a) // RUN, PACK, RUN])
+            nc.vector.tensor_tensor(rounded(a, b).rearrange("p (c s) j -> p c j s", s=RUN), staged(a, b).rearrange("p j (c s) -> p c j s", s=RUN), weights, MULT)
+
+        def round_on_gpsimd(a, b):
+            nc.gpsimd.tensor_scalar(rounded(a, b), staged(a, b).rearrange("p j s -> p s j"), 1.0, 0.0, MULT, ADD)
 
         codes = {}
         planes = {}
 
         def quantize(n):
             a, b = SPANS[n]
-            codes[n] = keep.tile([P, b - a], U32, name="codes%d" % n, tag="stage2" if n == 0 else "codes%d" % n, align_bytes=64)
+            codes[n] = keep.tile([P, b - a], U32, name="codes%d" % n, align_bytes=64)
             planes[n] = keep.tile([P, b - a], U8, name="plane%d" % n, align_bytes=64)
             nc.vector.quantize_mx(out=codes[n][:].bitcast(FP8X4), scales=planes[n][:], in_=rounded(a, b).rearrange("p s j -> p (s j)"))
 
-        BANKS = [[(0, 4), (4, 8), (8, 10), (10, 11), (11, 12)], [(0, 4), (4, 8), (8, 12)]]
-        TAGS = [["a", "c", "e", "f", "a"], ["b", "d", "g0"]]
-        banks = {}
-
-        def sums_bank(h, i):
-            if (h, i) not in banks:
-                banks[h, i] = bank(TAGS[h][i])
-            return banks[h, i]
-
-        def multiply(n, h):
-            for e in range(SPANS[n][0] // C, SPANS[n][1] // C):
-                i = [i for i, (lo, hi) in enumerate(BANKS[h]) if lo <= e < hi][0]
-                place = e - BANKS[h][i][0]
+        def multiply(target, h, first, end):
+            for e in range(first, end):
+                n = [n for n, (a, b) in enumerate(SPANS) if a <= e * C < b][0]
                 cols = slice(e * C - SPANS[n][0], (e + 1) * C - SPANS[n][0])
                 nc.tensor.matmul_mx(
-                    out=sums_bank(h, i)[:, place * C : (place + 1) * C],
+                    out=target[:, (e - first) * C : (e - first + 1) * C],
                     lhsT=w_codes[:, e, 2 * P * h : 2 * P * (h + 1)].bitcast(FP4X4),
                     lhsT_scale=w_plane[:, e, P * h : P * (h + 1)],
                     rhs=codes[n][:, cols].bitcast(FP8X4),
@@ -149,45 +128,62 @@ def tile_moe_pre_lin_none_kernel(tc, xT, w_words, w_scales, gate, offs, pos1, po
                     stop=True,
                 )
 
-        def empty(copy, h, i):
-            first, end = BANKS[h][i]
-            copy(y[h][:, first * C : end * C], sums_bank(h, i)[:, : (end - first) * C])
+        def empty(copy, source, h, first, end):
+            copy(y[h][:, first * C : end * C], source[:, : (end - first) * C])
 
         def gather(a, b):
             for j in range(PACK):
-                nc.scalar.activation(gathered[a][:, j, : b - a], window(j, a, b), COPY)
+                nc.scalar.activation(staged(a, b)[:, j, :], window(j, a, b), COPY)
+
+        def gather_weighed(rows, a, b, gates):
+            for j in rows:
+                nc.vector.tensor_tensor(staged(a, b)[:, j, :], window(j, a, b), gates[:], MULT)
 
         gather(a1, b1)
-        for j, (a, b) in [(0, GATE_CHUNKS[0]), (0, GATE_CHUNKS[1]), (1, (0, OWN)), (2, (0, OWN)), (3, (0, OWN))]:
-            nc.vector.tensor_tensor(gathered[0][:, j, a:b], window(j, a, b), gates(a, b), MULT)
+        gather_weighed((0, 1, 2, 3), 0, OWN, first_gates)
+        round_on_gpsimd(0, OWN)
+        stages[a2] = keep.tile([P, PACK * (b2 - a2)], F32, name="stage_second", tag="second_piece")[:]
         gather(a2, b2)
         gather(a3, b3)
-        nc.gpsimd.tensor_scalar(rounded(0, OWN), stage_own[:].rearrange("p j s -> p s j"), 1.0, 0.0, MULT, ADD)
-        weigh(a1, b1)
-        weigh(a2, b2)
-        quantize(1)
+        gather_weighed((0,), SPREAD_END, S, last_gates)
+        weigh(a1, 512)
+        weigh(512, b1)
+        gather_weighed((1,), SPREAD_END, S, last_gates)
         quantize(0)
+        gather_weighed((2, 3), SPREAD_END, S, last_gates)
+        round_on_gpsimd(SPREAD_END, S)
+        stages[a4] = keep.tile([P, PACK * (b4 - a4)], F32, name="stage_fourth", tag="fourth_piece")[:]
+        gather(a4, b4)
+        weigh(a2, 768)
+        weigh(768, b2)
+        quantize(1)
         quantize(2)
-        weigh(a3, 1408)
-        weigh(1408, b3)
+        weigh(a3, b3)
+        weigh(a4, b4)
         quantize(3)
         quantize(4)
-        for n in (1, 0):
-            multiply(n, 0)
-        for h, i in [(0, 1), (0, 0)]:
-            empty(nc.scalar.copy, h, i)
-        multiply(1, 1)
-        multiply(2, 0)
-        multiply(0, 1)
-        multiply(3, 0)
-        multiply(4, 0)
-        for i in (2, 3, 4):
-            empty(nc.scalar.copy, 0, i)
-        for n in (2, 3, 4):
-            multiply(n, 1)
-        empty(nc.scalar.copy, 1, 2)
-        for i in (1, 0):
-            empty(nc.vector.tensor_copy, 1, i)
+
+        a, b, c, d, e, f = [bank(tag) for tag in "abcdef"]
+        multiply(a, 0, 0, 4)
+        multiply(b, 1, 0, 4)
+        empty(nc.scalar.copy, a, 0, 0, 4)
+        g0 = bank("g0")
+        multiply(d, 0, 10, 12)
+        multiply(c, 0, 4, 7)
+        multiply(d[:, 2 * C :], 1, 10, 12)
+        multiply(g0, 1, 4, 7)
+        empty(nc.scalar.copy, d, 0, 10, 12)
+        empty(nc.scalar.copy, c, 0, 4, 7)
+        empty(nc.scalar.copy, b, 1, 0, 4)
+        multiply(e, 0, 7, 9)
+        multiply(f, 0, 9, 10)
+        empty(nc.vector.tensor_copy, g0, 1, 4, 7)
+        empty(nc.vector.tensor_copy, d[:, 2 * C :], 1, 10, 12)
+        empty(nc.scalar.copy, e, 0, 7, 9)
+        empty(nc.vector.tensor_copy, f, 0, 9, 10)
+        g1 = bank("g1")
+        multiply(g1, 1, 7, 10)
+        empty(nc.scalar.copy, g1, 1, 7, 10)
 
         def picked(h, r, a, b):
             return y[h][:].indirect(back_lists[r][:, a // 16 : b // 16])

@@ -43,7 +43,7 @@ def tile_moe_pre_lin_none_kernel(tc, xT, w_words, w_scales, gate, offs, pos1, po
         (a1, b1), (a2, b2), (a3, b3), (a4, b4) = PIECES
         first_gates = keep.tile([P, OWN], F32, name="first_gates", tag="second_piece")
         last_gates = keep.tile([P, OWN], F32, name="last_gates", tag="fourth_piece")
-        gate_columns = keep.tile([P, 2, 2 * RUN], F32, name="gate_columns")
+        gate_columns = [keep.tile([P, RUN], F32, name="gate_columns%d" % g) for g in range(2)]
         stage_own = keep.tile([P, PACK * OWN], F32, name="stage_own")
         stage_shared = keep.tile([P, OWN + PACK * (b1 - a1)], F32, name="stage_shared")
         identity = keep.tile([P, P], F32, name="identity")
@@ -66,11 +66,12 @@ def tile_moe_pre_lin_none_kernel(tc, xT, w_words, w_scales, gate, offs, pos1, po
         nc.sync.dma_start(x_rows[0][:, :T], x_hbm[:, 0, :])
         nc.sync.dma_start(slot_list[:], offs)
         nc.sync.dma_start(first_gates[:], gate_hbm[:, 0, :OWN])
-        for j in (1, 2):
+        for j in range(1, PACK):
             nc.sync.dma_start(x_rows[j][:, :T], x_hbm[:, j, :])
-        nc.sync.dma_start(gate_columns[:, :, :RUN], gate[0, OWN:SPREAD_END].rearrange("(g n b) -> n g b", g=2, b=RUN))
-        nc.sync.dma_start(x_rows[3][:, :T], x_hbm[:, 3, :])
+        columns_hbm = gate[0, OWN:SPREAD_END].rearrange("(g n b) -> g n b", g=2, b=RUN)
+        nc.sync.dma_start(gate_columns[0][:], columns_hbm[0])
         nc.sync.dma_start(last_gates[:], gate_hbm[:, 0, SPREAD_END:])
+        nc.sync.dma_start(gate_columns[1][:], columns_hbm[1])
         for q in range(4):
             nc.sync.dma_start(w_plane[32 * q : 32 * q + 4, :, :].bitcast(I32), scales_hbm[4 * q : 4 * q + 4, :, :].bitcast(I32))
         nc.sync.dma_start(w_codes[:].bitcast(I32), words_hbm.bitcast(I32))
@@ -81,7 +82,7 @@ def tile_moe_pre_lin_none_kernel(tc, xT, w_words, w_scales, gate, offs, pos1, po
         spread_gates = [bank("g0"), bank("g1")]
         for g in range(2):
             for b in range(RUN):
-                nc.tensor.transpose(spread_gates[g][:, b * P : (b + 1) * P], gate_columns[:, g, b : b + 1].to_broadcast([P, P]), identity[:])
+                nc.tensor.transpose(spread_gates[g][:, b * P : (b + 1) * P], gate_columns[g][:, b : b + 1].to_broadcast([P, P]), identity[:])
 
         stages = {0: stage_own[:], a1: stage_shared[:, OWN:], SPREAD_END: stage_shared[:, : PACK * OWN], a3: stage_own[:, : PACK * (b3 - a3)]}
         rounded_tile = keep.tile([P, 1024, PACK], BF16, name="rounded", align_bytes=64)
@@ -148,9 +149,8 @@ def tile_moe_pre_lin_none_kernel(tc, xT, w_words, w_scales, gate, offs, pos1, po
         gather_weighed((0,), SPREAD_END, S, last_gates)
         weigh(a1, 512)
         weigh(512, b1)
-        gather_weighed((1,), SPREAD_END, S, last_gates)
+        gather_weighed((1, 2, 3), SPREAD_END, S, last_gates)
         quantize(0)
-        gather_weighed((2, 3), SPREAD_END, S, last_gates)
         round_on_gpsimd(SPREAD_END, S)
         stages[a4] = keep.tile([P, PACK * (b4 - a4)], F32, name="stage_fourth", tag="fourth_piece")[:]
         gather(a4, b4)
@@ -164,20 +164,20 @@ def tile_moe_pre_lin_none_kernel(tc, xT, w_words, w_scales, gate, offs, pos1, po
         quantize(4)
 
         a, b, c, d, e, f = [bank(tag) for tag in "abcdef"]
-        multiply(a, 0, 0, 4)
-        multiply(b, 1, 0, 4)
-        empty(nc.scalar.copy, a, 0, 0, 4)
         g0 = bank("g0")
+        multiply(b, 1, 0, 4)
+        multiply(g0, 0, 0, 4)
+        empty(nc.scalar.copy, g0, 0, 0, 4)
         multiply(d, 0, 10, 12)
         multiply(c, 0, 4, 7)
         multiply(d[:, 2 * C :], 1, 10, 12)
-        multiply(g0, 1, 4, 7)
+        multiply(a, 1, 4, 7)
         empty(nc.scalar.copy, d, 0, 10, 12)
         empty(nc.scalar.copy, c, 0, 4, 7)
         empty(nc.scalar.copy, b, 1, 0, 4)
         multiply(e, 0, 7, 9)
         multiply(f, 0, 9, 10)
-        empty(nc.vector.tensor_copy, g0, 1, 4, 7)
+        empty(nc.vector.tensor_copy, a, 1, 4, 7)
         empty(nc.vector.tensor_copy, d[:, 2 * C :], 1, 10, 12)
         empty(nc.scalar.copy, e, 0, 7, 9)
         empty(nc.vector.tensor_copy, f, 0, 9, 10)

@@ -42,7 +42,8 @@ def tile_moe_pre_lin_none_kernel(tc, xT, w_words, w_scales, gate, offs, pos1, po
         x_rows = [keep.tile([P, WINDOW], F32, name="x_row%d" % j) for j in range(PACK)]
         (a1, b1), (a2, b2), (a3, b3), (a4, b4) = PIECES
         first_gates = keep.tile([P, OWN], F32, name="first_gates", tag="second_piece")
-        last_gates = keep.tile([P, OWN], F32, name="last_gates", tag="fourth_piece")
+        stage_fourth = keep.tile([P, PACK * (b4 - a4)], F32, name="stage_fourth")
+        last_gates = stage_fourth[:, 192 : 192 + OWN]
         gate_columns = [keep.tile([P, RUN], F32, name="gate_columns%d" % g) for g in range(2)]
         stage_own = keep.tile([P, PACK * OWN], F32, name="stage_own")
         stage_shared = keep.tile([P, OWN + PACK * (b1 - a1)], F32, name="stage_shared")
@@ -61,8 +62,8 @@ def tile_moe_pre_lin_none_kernel(tc, xT, w_words, w_scales, gate, offs, pos1, po
         words_hbm = w_words.rearrange("e a p b -> p (e a) b")
         scales_hbm = w_scales.rearrange("e a q n -> q (e a) n")
 
-        nc.vector.memset(w_plane[:, : E // 2, :].bitcast(U32), 0)
-        nc.scalar.copy(w_plane[:, E // 2 :, :].bitcast(U32), w_plane[:, : E // 2, :].bitcast(U32))
+        nc.vector.memset(w_plane[:, : E - 1, :].bitcast(U32), 0)
+        nc.scalar.copy(w_plane[:, E - 1, :].bitcast(U32), w_plane[:, 0, :].bitcast(U32))
         nc.sync.dma_start(x_rows[0][:, :T], x_hbm[:, 0, :])
         nc.sync.dma_start(slot_list[:], offs)
         nc.sync.dma_start(first_gates[:], gate_hbm[:, 0, :OWN])
@@ -70,7 +71,7 @@ def tile_moe_pre_lin_none_kernel(tc, xT, w_words, w_scales, gate, offs, pos1, po
             nc.sync.dma_start(x_rows[j][:, :T], x_hbm[:, j, :])
         columns_hbm = gate[0, OWN:SPREAD_END].rearrange("(g n b) -> g n b", g=2, b=RUN)
         nc.sync.dma_start(gate_columns[0][:], columns_hbm[0])
-        nc.sync.dma_start(last_gates[:], gate_hbm[:, 0, SPREAD_END:])
+        nc.sync.dma_start(last_gates, gate_hbm[:, 0, SPREAD_END:])
         nc.sync.dma_start(gate_columns[1][:], columns_hbm[1])
         for q in range(4):
             nc.sync.dma_start(w_plane[32 * q : 32 * q + 4, :, :].bitcast(I32), scales_hbm[4 * q : 4 * q + 4, :, :].bitcast(I32))
@@ -84,7 +85,7 @@ def tile_moe_pre_lin_none_kernel(tc, xT, w_words, w_scales, gate, offs, pos1, po
             for b in range(RUN):
                 nc.tensor.transpose(spread_gates[g][:, b * P : (b + 1) * P], gate_columns[g][:, b : b + 1].to_broadcast([P, P]), identity[:])
 
-        stages = {0: stage_own[:], a1: stage_shared[:, OWN:], SPREAD_END: stage_shared[:, : PACK * OWN], a3: stage_own[:, : PACK * (b3 - a3)]}
+        stages = {0: stage_own[:], a1: stage_shared[:, OWN:], SPREAD_END: stage_shared[:, : PACK * OWN], a3: stage_own[:, : PACK * (b3 - a3)], a4: stage_fourth[:]}
         rounded_tile = keep.tile([P, 1024, PACK], BF16, name="rounded", align_bytes=64)
 
         def rounded(a, b):
@@ -132,16 +133,17 @@ def tile_moe_pre_lin_none_kernel(tc, xT, w_words, w_scales, gate, offs, pos1, po
         def empty(copy, source, h, first, end):
             copy(y[h][:, first * C : end * C], source[:, : (end - first) * C])
 
-        def gather(a, b):
-            for j in range(PACK):
+        def gather(a, b, first_row=0):
+            for j in range(first_row, PACK):
                 nc.scalar.activation(staged(a, b)[:, j, :], window(j, a, b), COPY)
 
         def gather_weighed(rows, a, b, gates):
             for j in rows:
-                nc.vector.tensor_tensor(staged(a, b)[:, j, :], window(j, a, b), gates[:], MULT)
+                nc.vector.tensor_tensor(staged(a, b)[:, j, :], window(j, a, b), gates, MULT)
 
+        nc.vector.tensor_copy(staged(a4, b4)[:, 0, :], window(0, a4, b4))
         gather(a1, b1)
-        gather_weighed((0, 1, 2, 3), 0, OWN, first_gates)
+        gather_weighed((0, 1, 2, 3), 0, OWN, first_gates[:])
         round_on_gpsimd(0, OWN)
         stages[a2] = keep.tile([P, PACK * (b2 - a2)], F32, name="stage_second", tag="second_piece")[:]
         gather(a2, b2)
@@ -152,8 +154,7 @@ def tile_moe_pre_lin_none_kernel(tc, xT, w_words, w_scales, gate, offs, pos1, po
         gather_weighed((1, 2, 3), SPREAD_END, S, last_gates)
         quantize(0)
         round_on_gpsimd(SPREAD_END, S)
-        stages[a4] = keep.tile([P, PACK * (b4 - a4)], F32, name="stage_fourth", tag="fourth_piece")[:]
-        gather(a4, b4)
+        gather(a4, b4, 1)
         weigh(a2, 768)
         weigh(768, b2)
         quantize(1)
@@ -170,7 +171,7 @@ def tile_moe_pre_lin_none_kernel(tc, xT, w_words, w_scales, gate, offs, pos1, po
         empty(nc.scalar.copy, g0, 0, 0, 4)
         multiply(d, 0, 10, 12)
         multiply(c, 0, 4, 7)
-        multiply(d[:, 2 * C :], 1, 10, 12)
+        multiply(f[:, C:], 1, 10, 12)
         multiply(a, 1, 4, 7)
         empty(nc.scalar.copy, d, 0, 10, 12)
         empty(nc.scalar.copy, c, 0, 4, 7)
@@ -178,9 +179,9 @@ def tile_moe_pre_lin_none_kernel(tc, xT, w_words, w_scales, gate, offs, pos1, po
         multiply(e, 0, 7, 9)
         multiply(f, 0, 9, 10)
         empty(nc.vector.tensor_copy, a, 1, 4, 7)
-        empty(nc.vector.tensor_copy, d[:, 2 * C :], 1, 10, 12)
         empty(nc.scalar.copy, e, 0, 7, 9)
         empty(nc.vector.tensor_copy, f, 0, 9, 10)
+        empty(nc.vector.tensor_copy, f[:, C:], 1, 10, 12)
         g1 = bank("g1")
         multiply(g1, 1, 7, 10)
         empty(nc.scalar.copy, g1, 1, 7, 10)

@@ -86,10 +86,10 @@ def tile_moe_pre_lin_none_kernel(tc, xT, w_words, w_scales, gate, offs, pos1, po
                 nc.tensor.transpose(spread_gates[g][:, b * P : (b + 1) * P], gate_columns[g][:, b : b + 1].to_broadcast([P, P]), identity[:])
 
         stages = {0: stage_own[:], a1: stage_shared[:, OWN:], SPREAD_END: stage_shared[:, : PACK * OWN], a3: stage_own[:, : PACK * (b3 - a3)], a4: stage_fourth[:]}
-        rounded_tile = keep.tile([P, 1024, PACK], BF16, name="rounded", align_bytes=64)
+        rounded_tile = keep.tile([P, 1216, PACK], BF16, name="rounded", align_bytes=64)
 
         def rounded(a, b):
-            at = a + 192 if a < 512 else a - 512
+            at = a + 448 if a < 512 else (a - 512 if a < SPREAD_END else a - 320)
             return rounded_tile[:, at : at + b - a, :]
 
         def window(j, a, b):

@@ -189,24 +189,16 @@ def tile_moe_pre_lin_none_kernel(tc, xT, w_words, w_scales, gate, offs, pos1, po
         def picked(h, r, a, b):
             return y[h][:].indirect(back_lists[r][:, a // 16 : b // 16])
 
-        def fetch(h, r, a, b):
-            nc.scalar.activation(sums[h][r][:, a:b], picked(h, r, a, b), COPY)
-
-        def fetch_add(h, r, onto, a, b):
-            nc.vector.tensor_tensor(sums[h][r][:, a:b], picked(h, min(r, 2), a, b), sums[h][onto][:, a:b], ADD)
-
-        A = 192
-        nc.vector.tensor_copy(sums[0][0][:, :A], picked(0, 0, 0, A))
-        fetch(0, 0, A, T)
-        fetch(1, 0, 0, T)
-        fetch(0, 1, A, T)
-        fetch(1, 1, 0, 384)
-        fetch(1, 1, 384, T)
-        fetch_add(0, 1, 0, 0, A)
-        fetch_add(0, 2, 0, A, T)
-        fetch_add(0, 3, 1, 0, A)
-        nc.sync.dma_start(out[0:P, :A], sums[0][3][:, :A])
-        fetch_add(1, 2, 0, 0, T)
-        for h, a, b in [(0, A, T), (1, 0, 256), (1, 256, 384), (1, 384, T)]:
-            nc.vector.tensor_tensor(sums[h][3][:, a:b], sums[h][2][:, a:b], sums[h][1][:, a:b], ADD)
+        A, B = 384, 416
+        terms = keep.tile([P, B + T], F32, name="terms")
+        first = [terms[:, :T], sums[1][0][:]]
+        second = [terms[:, B:], sums[1][1][:]]
+        nc.vector.tensor_copy(first[0][:, :A], picked(0, 0, 0, A))
+        nc.scalar.activation(first[0][:, A:], picked(0, 0, A, T), COPY)
+        nc.scalar.activation(first[1], picked(1, 0, 0, T), COPY)
+        for h, a, b in [(0, B, T), (0, 0, B), (1, 0, T)]:
+            nc.vector.tensor_tensor(sums[h][2][:, a:b], picked(h, 2, a, b), first[h][:, a:b], ADD)
+        for h, a, b in [(0, 0, T), (1, 0, 320), (1, 320, T)]:
+            nc.scalar.activation(second[h][:, a:b], picked(h, 1, a, b), COPY)
+            nc.vector.tensor_tensor(sums[h][3][:, a:b], sums[h][2][:, a:b], second[h][:, a:b], ADD)
             nc.sync.dma_start(out[h * P : (h + 1) * P, a:b], sums[h][3][:, a:b])

@@ -171,20 +171,22 @@ def tile_moe_pre_lin_none_kernel(tc, xT, w_words, w_scales, gate, offs, pos1, po
         empty(nc.scalar.copy, g0, 0, 0, 4)
         multiply(d, 0, 10, 12)
         multiply(c, 0, 4, 7)
-        multiply(f[:, C:], 1, 10, 12)
+        multiply(d[:, 2 * C :], 1, 10, 12)
         multiply(a, 1, 4, 7)
         empty(nc.scalar.copy, d, 0, 10, 12)
         empty(nc.scalar.copy, c, 0, 4, 7)
         empty(nc.scalar.copy, b, 1, 0, 4)
+        empty(nc.scalar.copy, d[:, 2 * C :], 1, 10, 12)
         multiply(e, 0, 7, 9)
         multiply(f, 0, 9, 10)
         empty(nc.vector.tensor_copy, a, 1, 4, 7)
         empty(nc.scalar.copy, e, 0, 7, 9)
         empty(nc.vector.tensor_copy, f, 0, 9, 10)
-        empty(nc.vector.tensor_copy, f[:, C:], 1, 10, 12)
         g1 = bank("g1")
-        multiply(g1, 1, 7, 10)
-        empty(nc.scalar.copy, g1, 1, 7, 10)
+        multiply(g1, 1, 7, 9)
+        multiply(c[:, 3 * C :], 1, 9, 10)
+        empty(nc.scalar.copy, g1, 1, 7, 9)
+        empty(nc.vector.tensor_copy, c[:, 3 * C :], 1, 9, 10)
 
         def picked(h, r, a, b):
             return y[h][:].indirect(back_lists[r][:, a // 16 : b // 16])

@@ -22,11 +22,20 @@ MULT = mybir.AluOpType.mult
 ADD = mybir.AluOpType.add
 COPY = mybir.ActivationFunctionType.Copy
 
-OWN = 256
-SPREAD_END = 1280
-PIECES = [(OWN, 576), (576, 960), (960, 1152), (1152, SPREAD_END)]
-WINDOW = 528
-SPANS = [(0, 512), (SPREAD_END, S), (512, 896), (896, 1152), (1152, SPREAD_END)]
+FUSED = 320
+EARLY_POOL_END = 448
+LONG_FROM = 768
+EARLY_END = 896
+LATE_POOL = 1120
+LATE_POOL_END = 1280
+PITCH1 = EARLY_END - FUSED
+PITCH2 = 4 * PITCH1 + LATE_POOL_END - EARLY_END
+PITCH3 = 3 * PITCH2 + S - EARLY_END
+PITCHES = [(FUSED, PITCH1), (EARLY_END, PITCH2), (LATE_POOL_END, PITCH3)]
+ROW3 = 3 * PITCH3 - (LATE_POOL_END - FUSED)
+WINDOWS = (592, 592, 592, 784)
+SPANS = [(0, 384), (384, EARLY_END), (EARLY_END, 1280), (1280, S)]
+LATE_PLACE = 0
 RUN = 4
 
 
@@ -39,14 +48,19 @@ def tile_moe_pre_lin_none_kernel(tc, xT, w_words, w_scales, gate, offs, pos1, po
 
         slot_list = lists.tile([P, S // 16], U16, name="slot_list")
         back_lists = [lists.tile([P, T // 16], U16, name="back_list%d" % r) for r in range(3)]
-        x_rows = [keep.tile([P, WINDOW], F32, name="x_row%d" % j) for j in range(PACK)]
-        (a1, b1), (a2, b2), (a3, b3), (a4, b4) = PIECES
-        first_gates = keep.tile([P, OWN], F32, name="first_gates", tag="second_piece")
-        stage_fourth = keep.tile([P, PACK * (b4 - a4)], F32, name="stage_fourth")
-        last_gates = stage_fourth[:, 192 : 192 + OWN]
-        gate_columns = [keep.tile([P, RUN], F32, name="gate_columns%d" % g) for g in range(2)]
-        stage_own = keep.tile([P, PACK * OWN], F32, name="stage_own")
-        stage_shared = keep.tile([P, OWN + PACK * (b1 - a1)], F32, name="stage_shared")
+        x_rows = [keep.tile([P, WINDOWS[j]], F32, name="x_row%d" % j) for j in range(PACK)]
+        stage = keep.tile([P, 4 * PITCH3], F32, name="stage")
+
+        def staged(a, b):
+            first, pitch = [(f, p) for f, p in PITCHES if f <= a][-1]
+            at = ROW3 + first - FUSED - 3 * pitch
+            return stage[:, at : at + 4 * pitch].rearrange("p (j s) -> p j s", j=PACK)[:, :, a - first : b - first]
+
+        fused_gates = staged(EARLY_END, EARLY_END + FUSED)[:, 0, :]
+        fused_stage = keep.tile([P, PACK, FUSED], F32, name="fused_stage")
+        early_gates = keep.tile([P, EARLY_POOL_END - FUSED], F32, name="early_gates")
+        late_gates = keep.tile([P, LATE_POOL_END - LATE_POOL], F32, name="late_gates", tag="y1")
+        gate_columns = [staged(at, at + 2)[:, 1:3, :] for at in (EARLY_END, LATE_POOL_END)]
         identity = keep.tile([P, P], F32, name="identity")
 
         def bank(tag):
@@ -54,25 +68,27 @@ def tile_moe_pre_lin_none_kernel(tc, xT, w_words, w_scales, gate, offs, pos1, po
 
         w_codes = keep.tile([P, E, 2 * N], U8, name="w_codes", align_bytes=64)
         w_plane = keep.tile([P, E, N], U8, name="w_plane", align_bytes=64)
-        y = [keep.tile([P, S], F32, name="y%d" % h) for h in range(2)]
-        sums = [[keep.tile([P, T], F32, name="sum%d_%d" % (h, r)) for r in range(4)] for h in range(2)]
 
         x_hbm = xT.rearrange("(p j) t -> p j t", j=PACK)
         gate_hbm = gate.rearrange("(p j) s -> p j s", j=PACK)
         words_hbm = w_words.rearrange("e a p b -> p (e a) b")
         scales_hbm = w_scales.rearrange("e a q n -> q (e a) n")
 
+        def columns_hbm(a, b):
+            return gate[0, a:b].rearrange("(n u v) -> n u v", u=2, v=2)
+
         nc.vector.memset(w_plane[:, : E - 1, :].bitcast(U32), 0)
         nc.scalar.copy(w_plane[:, E - 1, :].bitcast(U32), w_plane[:, 0, :].bitcast(U32))
         nc.sync.dma_start(x_rows[0][:, :T], x_hbm[:, 0, :])
         nc.sync.dma_start(slot_list[:], offs)
-        nc.sync.dma_start(first_gates[:], gate_hbm[:, 0, :OWN])
+        nc.sync.dma_start(fused_gates, gate_hbm[:, 0, :FUSED])
         for j in range(1, PACK):
             nc.sync.dma_start(x_rows[j][:, :T], x_hbm[:, j, :])
-        columns_hbm = gate[0, OWN:SPREAD_END].rearrange("(g n b) -> g n b", g=2, b=RUN)
-        nc.sync.dma_start(gate_columns[0][:], columns_hbm[0])
-        nc.sync.dma_start(last_gates, gate_hbm[:, 0, SPREAD_END:])
-        nc.sync.dma_start(gate_columns[1][:], columns_hbm[1])
+        nc.sync.dma_start(gate_columns[0], columns_hbm(EARLY_END - 512, EARLY_END))
+        nc.sync.dma_start(early_gates[:], gate_hbm[:, 0, FUSED:EARLY_POOL_END])
+        nc.sync.dma_start(gate_columns[1][:64], columns_hbm(EARLY_END, EARLY_END + 256))
+        nc.sync.dma_start(gate_columns[1][64:], columns_hbm(S - 256, S))
+        nc.sync.dma_start(late_gates[:], gate_hbm[:, 0, LATE_POOL:LATE_POOL_END])
         for q in range(4):
             nc.sync.dma_start(w_plane[32 * q : 32 * q + 4, :, :].bitcast(I32), scales_hbm[4 * q : 4 * q + 4, :, :].bitcast(I32))
         nc.sync.dma_start(w_codes[:].bitcast(I32), words_hbm.bitcast(I32))
@@ -83,29 +99,30 @@ def tile_moe_pre_lin_none_kernel(tc, xT, w_words, w_scales, gate, offs, pos1, po
         spread_gates = [bank("g0"), bank("g1")]
         for g in range(2):
             for b in range(RUN):
-                nc.tensor.transpose(spread_gates[g][:, b * P : (b + 1) * P], gate_columns[g][:, b : b + 1].to_broadcast([P, P]), identity[:])
+                nc.tensor.transpose(spread_gates[g][:, b * P : (b + 1) * P], gate_columns[g][:, b // 2, b % 2 : b % 2 + 1].to_broadcast([P, P]), identity[:])
 
-        stages = {0: stage_own[:], a1: stage_shared[:, OWN:], SPREAD_END: stage_shared[:, : PACK * OWN], a3: stage_own[:, : PACK * (b3 - a3)], a4: stage_fourth[:]}
-        rounded_tile = keep.tile([P, 1216, PACK], BF16, name="rounded", align_bytes=64)
+        rounded_tile = keep.tile([P, EARLY_END, PACK], BF16, name="rounded", align_bytes=64)
 
         def rounded(a, b):
-            at = a + 448 if a < 512 else (a - 512 if a < SPREAD_END else a - 320)
+            at = a if a < EARLY_END else a - EARLY_END + LATE_PLACE
             return rounded_tile[:, at : at + b - a, :]
 
         def window(j, a, b):
             return x_rows[j][:].indirect(slot_list[:, a // 16 : b // 16])
 
-        def staged(a, b):
-            first = max(f for f in stages if f <= a)
-            return stages[first].rearrange("p (j s) -> p j s", j=PACK)[:, :, a - first : b - first]
+        def in_runs(engine, a, b, weights):
+            engine.tensor_tensor(
+                rounded(a, b).rearrange("p (c s) j -> p c j s", s=RUN),
+                staged(a, b).rearrange("p j (c s) -> p c j s", s=RUN),
+                weights.unsqueeze(2).to_broadcast([P, (b - a) // RUN, PACK, RUN]),
+                MULT,
+            )
 
-        def weigh(a, b):
-            g, at = divmod(a - OWN, 512)
-            weights = spread_gates[g][:].rearrange("p (s c) -> p c s", s=RUN)[:, at // RUN : (at + b - a) // RUN, :].unsqueeze(2).to_broadcast([P, (b - a) // RUN, PACK, RUN])
-            nc.vector.tensor_tensor(rounded(a, b).rearrange("p (c s) j -> p c j s", s=RUN), staged(a, b).rearrange("p j (c s) -> p c j s", s=RUN), weights, MULT)
+        def weigh(a, b, g, at):
+            in_runs(nc.vector, a, b, spread_gates[g][:].rearrange("p (s c) -> p c s", s=RUN)[:, at // RUN : (at + b - a) // RUN, :])
 
-        def round_on_gpsimd(a, b):
-            nc.gpsimd.tensor_scalar(rounded(a, b), staged(a, b).rearrange("p j s -> p s j"), 1.0, 0.0, MULT, ADD)
+        def weigh_on_gpsimd(a, b, gates):
+            in_runs(nc.gpsimd, a, b, gates[:].rearrange("p (c s) -> p c s", s=RUN))
 
         codes = {}
         planes = {}
@@ -130,77 +147,85 @@ def tile_moe_pre_lin_none_kernel(tc, xT, w_words, w_scales, gate, offs, pos1, po
                     stop=True,
                 )
 
+        def gather(j, a, b):
+            nc.scalar.activation(staged(a, b)[:, j, :], window(j, a, b), COPY)
+
+        nc.vector.tensor_copy(staged(LATE_POOL_END, S)[:, 0, :], window(0, LATE_POOL_END, S))
+        for j in range(PACK):
+            gather(j, FUSED, EARLY_END if j < 3 else LONG_FROM)
+            nc.vector.tensor_tensor(fused_stage[:, j, :], window(j, 0, FUSED), fused_gates, MULT)
+        nc.vector.tensor_copy(stage[:, ROW3 + LONG_FROM - FUSED : ROW3 + S - FUSED], window(3, LONG_FROM, S))
+        nc.gpsimd.tensor_scalar(rounded(0, FUSED), fused_stage[:].rearrange("p j s -> p s j"), 1.0, 0.0, MULT, ADD)
+        weigh_on_gpsimd(FUSED, EARLY_POOL_END, early_gates)
+        weigh(EARLY_POOL_END, EARLY_END, 0, EARLY_POOL_END - (EARLY_END - 512))
+        for j in range(3):
+            gather(j, EARLY_END, LATE_POOL_END)
+        for j in (1, 2):
+            gather(j, LATE_POOL_END, S)
+        quantize(0)
+        quantize(1)
+        weigh_on_gpsimd(LATE_POOL, LATE_POOL_END, late_gates)
+        weigh(EARLY_END, LATE_POOL, 1, 0)
+        weigh(LATE_POOL_END, S, 1, 512 - (S - LATE_POOL_END))
+        quantize(2)
+        quantize(3)
+
+        y = [keep.tile([P, S], F32, name="y0"), keep.tile([P, S], F32, name="y1", tag="y1")]
+
         def empty(copy, source, h, first, end):
             copy(y[h][:, first * C : end * C], source[:, : (end - first) * C])
 
-        def gather(a, b, first_row=0):
-            for j in range(first_row, PACK):
-                nc.scalar.activation(staged(a, b)[:, j, :], window(j, a, b), COPY)
-
-        def gather_weighed(rows, a, b, gates):
-            for j in rows:
-                nc.vector.tensor_tensor(staged(a, b)[:, j, :], window(j, a, b), gates, MULT)
-
-        nc.vector.tensor_copy(staged(a4, b4)[:, 0, :], window(0, a4, b4))
-        gather(a1, b1)
-        gather_weighed((0, 1, 2, 3), 0, OWN, first_gates[:])
-        round_on_gpsimd(0, OWN)
-        stages[a2] = keep.tile([P, PACK * (b2 - a2)], F32, name="stage_second", tag="second_piece")[:]
-        gather(a2, b2)
-        gather(a3, b3)
-        gather_weighed((0,), SPREAD_END, S, last_gates)
-        weigh(a1, 512)
-        weigh(512, b1)
-        gather_weighed((1, 2, 3), SPREAD_END, S, last_gates)
-        quantize(0)
-        round_on_gpsimd(SPREAD_END, S)
-        gather(a4, b4, 1)
-        weigh(a2, 768)
-        weigh(768, b2)
-        quantize(1)
-        quantize(2)
-        weigh(a3, b3)
-        weigh(a4, b4)
-        quantize(3)
-        quantize(4)
-
-        a, b, c, d, e, f = [bank(tag) for tag in "abcdef"]
+        a, b, c, d, f = [bank(tag) for tag in "abcdf"]
         g0 = bank("g0")
-        multiply(b, 1, 0, 4)
-        multiply(g0, 0, 0, 4)
-        empty(nc.scalar.copy, g0, 0, 0, 4)
-        multiply(d, 0, 10, 12)
-        multiply(c, 0, 4, 7)
-        multiply(d[:, 2 * C :], 1, 10, 12)
-        multiply(a, 1, 4, 7)
-        empty(nc.scalar.copy, d, 0, 10, 12)
-        empty(nc.scalar.copy, c, 0, 4, 7)
-        empty(nc.scalar.copy, b, 1, 0, 4)
-        empty(nc.scalar.copy, d[:, 2 * C :], 1, 10, 12)
-        multiply(e, 0, 7, 9)
-        multiply(f, 0, 9, 10)
-        empty(nc.vector.tensor_copy, a, 1, 4, 7)
-        empty(nc.scalar.copy, e, 0, 7, 9)
-        empty(nc.vector.tensor_copy, f, 0, 9, 10)
+        multiply(g0, 0, 0, 3)
+        multiply(a, 0, 3, 7)
+        multiply(b, 1, 0, 3)
+        multiply(c, 1, 3, 7)
         g1 = bank("g1")
-        multiply(g1, 1, 7, 9)
-        multiply(c[:, 3 * C :], 1, 9, 10)
-        empty(nc.scalar.copy, g1, 1, 7, 9)
-        empty(nc.vector.tensor_copy, c[:, 3 * C :], 1, 9, 10)
+        multiply(g1, 0, 7, 10)
+        multiply(d, 0, 10, 12)
+        multiply(f, 1, 10, 12)
+        empty(nc.scalar.copy, g0, 0, 0, 3)
+        empty(nc.scalar.copy, a, 0, 3, 7)
+        empty(nc.scalar.copy, b, 1, 0, 3)
+        empty(nc.vector.tensor_copy, c, 1, 3, 7)
+        empty(nc.scalar.copy, g1, 0, 7, 10)
+        e = bank("g1")
+        multiply(e, 1, 7, 10)
+        empty(nc.vector.tensor_copy, d, 0, 10, 12)
+        empty(nc.vector.tensor_copy, f, 1, 10, 12)
+        empty(nc.vector.tensor_copy, e, 1, 7, 10)
 
         def picked(h, r, a, b):
             return y[h][:].indirect(back_lists[r][:, a // 16 : b // 16])
 
-        A, B = 384, 416
-        terms = keep.tile([P, B + T], F32, name="terms")
-        first = [terms[:, :T], sums[1][0][:]]
-        second = [terms[:, B:], sums[1][1][:]]
-        nc.vector.tensor_copy(first[0][:, :A], picked(0, 0, 0, A))
-        nc.scalar.activation(first[0][:, A:], picked(0, 0, A, T), COPY)
-        nc.scalar.activation(first[1], picked(1, 0, 0, T), COPY)
-        for h, a, b in [(0, B, T), (0, 0, B), (1, 0, T)]:
-            nc.vector.tensor_tensor(sums[h][2][:, a:b], picked(h, 2, a, b), first[h][:, a:b], ADD)
-        for h, a, b in [(0, 0, T), (1, 0, 320), (1, 320, T)]:
-            nc.scalar.activation(second[h][:, a:b], picked(h, 1, a, b), COPY)
-            nc.vector.tensor_tensor(sums[h][3][:, a:b], sums[h][2][:, a:b], second[h][:, a:b], ADD)
-            nc.sync.dma_start(out[h * P : (h + 1) * P, a:b], sums[h][3][:, a:b])
+        H, CUT = T // 2, 320
+        first = [keep.tile([P, T], F32, name="first%d" % h) for h in range(2)]
+        two = [keep.tile([P, T], F32, name="two%d" % h) for h in range(2)]
+        second1 = keep.tile([P, T], F32, name="second1")
+        total = [keep.tile([P, T], F32, name="total%d" % h) for h in range(2)]
+
+        def fetch(target, h, r, a, b):
+            nc.scalar.activation(target, picked(h, r, a, b), COPY)
+
+        def fetch_add(target, h, r, a, b, other):
+            nc.vector.tensor_tensor(target[h][:, a:b], picked(h, r, a, b), other[h][:, a:b], ADD)
+
+        def store(h, a, b):
+            nc.sync.dma_start(out[h * P : (h + 1) * P, a:b], total[h][:, a:b])
+
+        fetch(first[0][:, :H], 0, 0, 0, H)
+        fetch(first[0][:, H:], 0, 0, H, T)
+        fetch(first[1][:], 1, 0, 0, T)
+        fetch_add(two, 0, 1, 0, H, first)
+        fetch_add(two, 0, 2, H, T, first)
+        fetch_add(total, 0, 2, 0, H, two)
+        store(0, 0, H)
+        fetch_add(two, 1, 2, 0, T, first)
+        fetch(first[0][:, :H], 0, 1, H, T)
+        nc.vector.tensor_tensor(total[0][:, H:], two[0][:, H:], first[0][:, :H], ADD)
+        store(0, H, T)
+        for a, b in [(0, CUT), (CUT, T)]:
+            fetch(second1[:, a:b], 1, 1, a, b)
+            nc.vector.tensor_tensor(total[1][:, a:b], two[1][:, a:b], second1[:, a:b], ADD)
+            store(1, a, b)

@@ -23,19 +23,14 @@ ADD = mybir.AluOpType.add
 COPY = mybir.ActivationFunctionType.Copy
 
 FUSED = 320
-EARLY_POOL_END = 448
-LONG_FROM = 768
-EARLY_END = 896
-LATE_POOL = 1120
-LATE_POOL_END = 1280
-PITCH1 = EARLY_END - FUSED
-PITCH2 = 4 * PITCH1 + LATE_POOL_END - EARLY_END
-PITCH3 = 3 * PITCH2 + S - EARLY_END
-PITCHES = [(FUSED, PITCH1), (EARLY_END, PITCH2), (LATE_POOL_END, PITCH3)]
-ROW3 = 3 * PITCH3 - (LATE_POOL_END - FUSED)
-WINDOWS = (592, 592, 592, 784)
-SPANS = [(0, 384), (384, EARLY_END), (EARLY_END, 1280), (1280, S)]
-LATE_PLACE = 0
+EARLY_POOL_END = 480
+EARLY_CUT = 896
+EARLY_END = 1024
+LATE_POOL = 1296
+LAST = 1408
+WINDOW = 720
+SPANS = [(0, 512), (512, EARLY_END), (EARLY_END, LAST), (LAST, S)]
+LATE_PLACE = 128
 RUN = 4
 
 
@@ -48,19 +43,19 @@ def tile_moe_pre_lin_none_kernel(tc, xT, w_words, w_scales, gate, offs, pos1, po
 
         slot_list = lists.tile([P, S // 16], U16, name="slot_list")
         back_lists = [lists.tile([P, T // 16], U16, name="back_list%d" % r) for r in range(3)]
-        x_rows = [keep.tile([P, WINDOWS[j]], F32, name="x_row%d" % j) for j in range(PACK)]
-        stage = keep.tile([P, 4 * PITCH3], F32, name="stage")
+        x_rows = [keep.tile([P, WINDOW], F32, name="x_row%d" % j) for j in range(PACK)]
+        waves = [(a, keep.tile([P, PACK, b - a], F32, name="wave%d" % a)) for a, b in [(FUSED, EARLY_END), (EARLY_END, LAST), (LAST, S)]]
 
         def staged(a, b):
-            first, pitch = [(f, p) for f, p in PITCHES if f <= a][-1]
-            at = ROW3 + first - FUSED - 3 * pitch
-            return stage[:, at : at + 4 * pitch].rearrange("p (j s) -> p j s", j=PACK)[:, :, a - first : b - first]
+            first, rows = [wave for wave in waves if wave[0] <= a][-1]
+            return rows[:, :, a - first : b - first]
 
         fused_gates = staged(EARLY_END, EARLY_END + FUSED)[:, 0, :]
         fused_stage = keep.tile([P, PACK, FUSED], F32, name="fused_stage")
         early_gates = keep.tile([P, EARLY_POOL_END - FUSED], F32, name="early_gates")
-        late_gates = keep.tile([P, LATE_POOL_END - LATE_POOL], F32, name="late_gates", tag="y1")
-        gate_columns = [staged(at, at + 2)[:, 1:3, :] for at in (EARLY_END, LATE_POOL_END)]
+        late_gates = keep.tile([P, LAST - LATE_POOL], F32, name="late_gates", tag="y1")
+        gate_columns = [staged(at, at + 2)[:, 1:3, :] for at in (EARLY_END, LAST)]
+        gate_column = staged(LAST, LAST + 1)[:, 3, :]
         identity = keep.tile([P, P], F32, name="identity")
 
         def bank(tag):
@@ -84,11 +79,11 @@ def tile_moe_pre_lin_none_kernel(tc, xT, w_words, w_scales, gate, offs, pos1, po
         nc.sync.dma_start(fused_gates, gate_hbm[:, 0, :FUSED])
         for j in range(1, PACK):
             nc.sync.dma_start(x_rows[j][:, :T], x_hbm[:, j, :])
-        nc.sync.dma_start(gate_columns[0], columns_hbm(EARLY_END - 512, EARLY_END))
+        nc.sync.dma_start(gate_columns[0], columns_hbm(EARLY_CUT - 512, EARLY_CUT))
         nc.sync.dma_start(early_gates[:], gate_hbm[:, 0, FUSED:EARLY_POOL_END])
-        nc.sync.dma_start(gate_columns[1][:64], columns_hbm(EARLY_END, EARLY_END + 256))
-        nc.sync.dma_start(gate_columns[1][64:], columns_hbm(S - 256, S))
-        nc.sync.dma_start(late_gates[:], gate_hbm[:, 0, LATE_POOL:LATE_POOL_END])
+        nc.sync.dma_start(gate_column, gate[0, EARLY_CUT:EARLY_END].rearrange("(n u) -> n u", u=1))
+        nc.sync.dma_start(gate_columns[1], columns_hbm(EARLY_END, S))
+        nc.sync.dma_start(late_gates[:], gate_hbm[:, 0, LATE_POOL:LAST])
         for q in range(4):
             nc.sync.dma_start(w_plane[32 * q : 32 * q + 4, :, :].bitcast(I32), scales_hbm[4 * q : 4 * q + 4, :, :].bitcast(I32))
         nc.sync.dma_start(w_codes[:].bitcast(I32), words_hbm.bitcast(I32))
@@ -96,10 +91,15 @@ def tile_moe_pre_lin_none_kernel(tc, xT, w_words, w_scales, gate, offs, pos1, po
             nc.sync.dma_start(tile[:], pos)
 
         make_identity(nc, identity[:])
-        spread_gates = [bank("g0"), bank("g1")]
-        for g in range(2):
+        spread_gates = [bank("g0"), bank("g1"), bank("g2")]
+
+        def spread(g):
             for b in range(RUN):
                 nc.tensor.transpose(spread_gates[g][:, b * P : (b + 1) * P], gate_columns[g][:, b // 2, b % 2 : b % 2 + 1].to_broadcast([P, P]), identity[:])
+
+        spread(0)
+        nc.tensor.transpose(spread_gates[2][:, :P], gate_column.to_broadcast([P, P]), identity[:])
+        spread(1)
 
         rounded_tile = keep.tile([P, EARLY_END, PACK], BF16, name="rounded", align_bytes=64)
 
@@ -150,23 +150,25 @@ def tile_moe_pre_lin_none_kernel(tc, xT, w_words, w_scales, gate, offs, pos1, po
         def gather(j, a, b):
             nc.scalar.activation(staged(a, b)[:, j, :], window(j, a, b), COPY)
 
-        nc.vector.tensor_copy(staged(LATE_POOL_END, S)[:, 0, :], window(0, LATE_POOL_END, S))
+        nc.vector.tensor_copy(staged(LAST, S)[:, 0, :], window(0, LAST, S))
         for j in range(PACK):
-            gather(j, FUSED, EARLY_END if j < 3 else LONG_FROM)
+            if j < 3:
+                gather(j, FUSED, EARLY_END)
             nc.vector.tensor_tensor(fused_stage[:, j, :], window(j, 0, FUSED), fused_gates, MULT)
-        nc.vector.tensor_copy(stage[:, ROW3 + LONG_FROM - FUSED : ROW3 + S - FUSED], window(3, LONG_FROM, S))
+        nc.vector.tensor_copy(staged(FUSED, EARLY_END)[:, 3, :], window(3, FUSED, EARLY_END))
         nc.gpsimd.tensor_scalar(rounded(0, FUSED), fused_stage[:].rearrange("p j s -> p s j"), 1.0, 0.0, MULT, ADD)
         weigh_on_gpsimd(FUSED, EARLY_POOL_END, early_gates)
-        weigh(EARLY_POOL_END, EARLY_END, 0, EARLY_POOL_END - (EARLY_END - 512))
-        for j in range(3):
-            gather(j, EARLY_END, LATE_POOL_END)
-        for j in (1, 2):
-            gather(j, LATE_POOL_END, S)
+        weigh(EARLY_POOL_END, EARLY_CUT, 0, EARLY_POOL_END - (EARLY_CUT - 512))
+        in_runs(nc.vector, EARLY_CUT, EARLY_END, spread_gates[2][:, :P].rearrange("p (c s) -> p c s", s=RUN))
+        for j in range(PACK):
+            gather(j, EARLY_END, LAST)
+        for j in range(1, PACK):
+            gather(j, LAST, S)
         quantize(0)
         quantize(1)
-        weigh_on_gpsimd(LATE_POOL, LATE_POOL_END, late_gates)
+        weigh_on_gpsimd(LATE_POOL, LAST, late_gates)
         weigh(EARLY_END, LATE_POOL, 1, 0)
-        weigh(LATE_POOL_END, S, 1, 512 - (S - LATE_POOL_END))
+        weigh(LAST, S, 1, LAST - EARLY_END)
         quantize(2)
         quantize(3)
 
@@ -175,57 +177,41 @@ def tile_moe_pre_lin_none_kernel(tc, xT, w_words, w_scales, gate, offs, pos1, po
         def empty(copy, source, h, first, end):
             copy(y[h][:, first * C : end * C], source[:, : (end - first) * C])
 
-        a, b, c, d, f = [bank(tag) for tag in "abcdf"]
+        a, b, c, d, e = [bank(tag) for tag in "abcde"]
         g0 = bank("g0")
-        multiply(g0, 0, 0, 3)
-        multiply(a, 0, 3, 7)
-        multiply(b, 1, 0, 3)
-        multiply(c, 1, 3, 7)
+        multiply(g0, 0, 0, 4)
+        multiply(a, 0, 4, 8)
+        multiply(b, 1, 0, 4)
+        multiply(c, 1, 4, 8)
         g1 = bank("g1")
-        multiply(g1, 0, 7, 10)
+        multiply(g1, 0, 8, 10)
         multiply(d, 0, 10, 12)
-        multiply(f, 1, 10, 12)
-        empty(nc.scalar.copy, g0, 0, 0, 3)
-        empty(nc.scalar.copy, a, 0, 3, 7)
-        empty(nc.scalar.copy, b, 1, 0, 3)
-        empty(nc.vector.tensor_copy, c, 1, 3, 7)
-        empty(nc.scalar.copy, g1, 0, 7, 10)
-        e = bank("g1")
-        multiply(e, 1, 7, 10)
+        g2 = bank("g2")
+        multiply(g2, 1, 8, 10)
+        multiply(e, 1, 10, 12)
+        empty(nc.scalar.copy, g0, 0, 0, 4)
+        empty(nc.scalar.copy, a, 0, 4, 8)
+        empty(nc.scalar.copy, b, 1, 0, 4)
+        empty(nc.vector.tensor_copy, c, 1, 4, 8)
+        empty(nc.scalar.copy, g1, 0, 8, 10)
         empty(nc.vector.tensor_copy, d, 0, 10, 12)
-        empty(nc.vector.tensor_copy, f, 1, 10, 12)
-        empty(nc.vector.tensor_copy, e, 1, 7, 10)
+        empty(nc.scalar.copy, g2, 1, 8, 10)
+        empty(nc.vector.tensor_copy, e, 1, 10, 12)
 
         def picked(h, r, a, b):
             return y[h][:].indirect(back_lists[r][:, a // 16 : b // 16])
 
-        H, CUT = T // 2, 320
-        first = [keep.tile([P, T], F32, name="first%d" % h) for h in range(2)]
-        two = [keep.tile([P, T], F32, name="two%d" % h) for h in range(2)]
-        second1 = keep.tile([P, T], F32, name="second1")
-        total = [keep.tile([P, T], F32, name="total%d" % h) for h in range(2)]
-
-        def fetch(target, h, r, a, b):
-            nc.scalar.activation(target, picked(h, r, a, b), COPY)
-
-        def fetch_add(target, h, r, a, b, other):
-            nc.vector.tensor_tensor(target[h][:, a:b], picked(h, r, a, b), other[h][:, a:b], ADD)
-
-        def store(h, a, b):
-            nc.sync.dma_start(out[h * P : (h + 1) * P, a:b], total[h][:, a:b])
-
-        fetch(first[0][:, :H], 0, 0, 0, H)
-        fetch(first[0][:, H:], 0, 0, H, T)
-        fetch(first[1][:], 1, 0, 0, T)
-        fetch_add(two, 0, 1, 0, H, first)
-        fetch_add(two, 0, 2, H, T, first)
-        fetch_add(total, 0, 2, 0, H, two)
-        store(0, 0, H)
-        fetch_add(two, 1, 2, 0, T, first)
-        fetch(first[0][:, :H], 0, 1, H, T)
-        nc.vector.tensor_tensor(total[0][:, H:], two[0][:, H:], first[0][:, :H], ADD)
-        store(0, H, T)
-        for a, b in [(0, CUT), (CUT, T)]:
-            fetch(second1[:, a:b], 1, 1, a, b)
-            nc.vector.tensor_tensor(total[1][:, a:b], two[1][:, a:b], second1[:, a:b], ADD)
-            store(1, a, b)
+        sums = [[keep.tile([P, T], F32, name="sum%d_%d" % (h, r)) for r in range(4)] for h in range(2)]
+        A, B = 384, 416
+        terms = keep.tile([P, B + T], F32, name="terms")
+        first = [terms[:, :T], sums[1][0][:]]
+        second = [terms[:, B:], sums[1][1][:]]
+        nc.vector.tensor_copy(first[0][:, :A], picked(0, 0, 0, A))
+        nc.scalar.activation(first[0][:, A:], picked(0, 0, A, T), COPY)
+        nc.scalar.activation(first[1], picked(1, 0, 0, T), COPY)
+        for h, a, b in [(0, B, T), (0, 0, B), (1, 0, T)]:
+            nc.vector.tensor_tensor(sums[h][2][:, a:b], picked(h, 2, a, b), first[h][:, a:b], ADD)
+        for h, a, b in [(0, 0, T), (1, 0, 320), (1, 320, T)]:
+            nc.scalar.activation(second[h][:, a:b], picked(h, 1, a, b), COPY)
+            nc.vector.tensor_tensor(sums[h][3][:, a:b], sums[h][2][:, a:b], second[h][:, a:b], ADD)
+            nc.sync.dma_start(out[h * P : (h + 1) * P, a:b], sums[h][3][:, a:b])

@@ -211,7 +211,8 @@ def tile_moe_pre_lin_none_kernel(tc, xT, w_words, w_scales, gate, offs, pos1, po
         nc.scalar.activation(first[1], picked(1, 0, 0, T), COPY)
         for h, a, b in [(0, B, T), (0, 0, B), (1, 0, T)]:
             nc.vector.tensor_tensor(sums[h][2][:, a:b], picked(h, 2, a, b), first[h][:, a:b], ADD)
-        for h, a, b in [(0, 0, T), (1, 0, 320), (1, 320, T)]:
+        for h, a, b, cuts in [(0, 0, T, (0, 256, T)), (1, 0, 320, (0, 320)), (1, 320, T, (320, T))]:
             nc.scalar.activation(second[h][:, a:b], picked(h, 1, a, b), COPY)
-            nc.vector.tensor_tensor(sums[h][3][:, a:b], sums[h][2][:, a:b], second[h][:, a:b], ADD)
-            nc.sync.dma_start(out[h * P : (h + 1) * P, a:b], sums[h][3][:, a:b])
+            for lo, hi in zip(cuts, cuts[1:]):
+                nc.vector.tensor_tensor(sums[h][3][:, lo:hi], sums[h][2][:, lo:hi], second[h][:, lo:hi], ADD)
+                nc.sync.dma_start(out[h * P : (h + 1) * P, lo:hi], sums[h][3][:, lo:hi])

from contextlib import ExitStack

import concourse.mybir as mybir
from concourse.masks import make_identity

K, T, E, C, N = 512, 512, 12, 128, 256
S = E * C
P = 128
PACK = 4
FLOPS = 2 * K * N * S
BYTES = 4 * K * T + E * P * 2 * N + E * 16 * N + 4 * S + 2 * P * (S + 3 * T) // 16 + 4 * N * T

F32 = mybir.dt.float32
BF16 = mybir.dt.bfloat16
I32 = mybir.dt.int32
U32 = mybir.dt.uint32
U16 = mybir.dt.uint16
U8 = mybir.dt.uint8
FP8X4 = mybir.dt.float8_e4m3fn_x4
FP4X4 = mybir.dt.float4_e2m1fn_x4
MULT = mybir.AluOpType.mult
ADD = mybir.AluOpType.add
COPY = mybir.ActivationFunctionType.Copy

FUSED = 320
EARLY_POOL_END = 480
EARLY_CUT = 896
EARLY_END = 1024
LATE_POOL = 1296
LAST = 1408
WINDOW = 720
SPANS = [(0, 512), (512, EARLY_END), (EARLY_END, LAST), (LAST, S)]
LATE_PLACE = 128
RUN = 4


def tile_moe_pre_lin_none_kernel(tc, xT, w_words, w_scales, gate, offs, pos1, pos2, pos3, out):
    nc = tc.nc
    with ExitStack() as ctx:
        lists = ctx.enter_context(tc.tile_pool(name="lists", bufs=1))
        keep = ctx.enter_context(tc.tile_pool(name="keep", bufs=1))
        psum = ctx.enter_context(tc.psum_pool(name="psum", bufs=1))

        slot_list = lists.tile([P, S // 16], U16, name="slot_list")
        back_lists = [lists.tile([P, T // 16], U16, name="back_list%d" % r) for r in range(3)]
        x_rows = [keep.tile([P, WINDOW], F32, name="x_row%d" % j) for j in range(PACK)]
        waves = [(a, keep.tile([P, PACK, b - a], F32, name="wave%d" % a)) for a, b in [(FUSED, EARLY_END), (EARLY_END, LAST), (LAST, S)]]

        def staged(a, b):
            first, rows = [wave for wave in waves if wave[0] <= a][-1]
            return rows[:, :, a - first : b - first]

        fused_gates = staged(EARLY_END, EARLY_END + FUSED)[:, 0, :]
        fused_stage = keep.tile([P, PACK, FUSED], F32, name="fused_stage")
        early_gates = keep.tile([P, EARLY_POOL_END - FUSED], F32, name="early_gates")
        late_gates = keep.tile([P, LAST - LATE_POOL], F32, name="late_gates", tag="y1")
        gate_columns = [staged(at, at + 2)[:, 1:3, :] for at in (EARLY_END, LAST)]
        gate_column = staged(LAST, LAST + 1)[:, 3, :]
        identity = keep.tile([P, P], F32, name="identity")

        def bank(tag):
            return psum.tile([P, 512], F32, name=tag, tag=tag)

        w_codes = keep.tile([P, E, 2 * N], U8, name="w_codes", align_bytes=64)
        w_plane = keep.tile([P, E, N], U8, name="w_plane", align_bytes=64)

        x_hbm = xT.rearrange("(p j) t -> p j t", j=PACK)
        gate_hbm = gate.rearrange("(p j) s -> p j s", j=PACK)
        words_hbm = w_words.rearrange("e a p b -> p (e a) b")
        scales_hbm = w_scales.rearrange("e a q n -> q (e a) n")

        def columns_hbm(a, b):
            return gate[0, a:b].rearrange("(n u v) -> n u v", u=2, v=2)

        nc.vector.memset(w_plane[:, : E - 1, :].bitcast(U32), 0)
        nc.scalar.copy(w_plane[:, E - 1, :].bitcast(U32), w_plane[:, 0, :].bitcast(U32))
        nc.sync.dma_start(x_rows[0][:, :T], x_hbm[:, 0, :])
        nc.sync.dma_start(slot_list[:], offs)
        nc.sync.dma_start(fused_gates, gate_hbm[:, 0, :FUSED])
        for j in range(1, PACK):
            nc.sync.dma_start(x_rows[j][:, :T], x_hbm[:, j, :])
        nc.sync.dma_start(gate_columns[0], columns_hbm(EARLY_CUT - 512, EARLY_CUT))
        nc.sync.dma_start(early_gates[:], gate_hbm[:, 0, FUSED:EARLY_POOL_END])
        nc.sync.dma_start(gate_column, gate[0, EARLY_CUT:EARLY_END].rearrange("(n u) -> n u", u=1))
        nc.sync.dma_start(gate_columns[1], columns_hbm(EARLY_END, S))
        nc.sync.dma_start(late_gates[:], gate_hbm[:, 0, LATE_POOL:LAST])
        for q in range(4):
            nc.sync.dma_start(w_plane[32 * q : 32 * q + 4, :, :].bitcast(I32), scales_hbm[4 * q : 4 * q + 4, :, :].bitcast(I32))
        nc.sync.dma_start(w_codes[:].bitcast(I32), words_hbm.bitcast(I32))
        for tile, pos in zip(back_lists, (pos1, pos2, pos3)):
            nc.sync.dma_start(tile[:], pos)

        make_identity(nc, identity[:])
        spread_gates = [bank("g0"), bank("g1"), bank("g2")]

        def spread(g):
            for b in range(RUN):
                nc.tensor.transpose(spread_gates[g][:, b * P : (b + 1) * P], gate_columns[g][:, b // 2, b % 2 : b % 2 + 1].to_broadcast([P, P]), identity[:])

        spread(0)
        nc.tensor.transpose(spread_gates[2][:, :P], gate_column.to_broadcast([P, P]), identity[:])
        spread(1)

        rounded_tile = keep.tile([P, EARLY_END, PACK], BF16, name="rounded", align_bytes=64)

        def rounded(a, b):
            at = a if a < EARLY_END else a - EARLY_END + LATE_PLACE
            return rounded_tile[:, at : at + b - a, :]

        def window(j, a, b):
            return x_rows[j][:].indirect(slot_list[:, a // 16 : b // 16])

        def in_runs(engine, a, b, weights):
            engine.tensor_tensor(
                rounded(a, b).rearrange("p (c s) j -> p c j s", s=RUN),
                staged(a, b).rearrange("p j (c s) -> p c j s", s=RUN),
                weights.unsqueeze(2).to_broadcast([P, (b - a) // RUN, PACK, RUN]),
                MULT,
            )

        def weigh(a, b, g, at):
            in_runs(nc.vector, a, b, spread_gates[g][:].rearrange("p (s c) -> p c s", s=RUN)[:, at // RUN : (at + b - a) // RUN, :])

        def weigh_on_gpsimd(a, b, gates):
            in_runs(nc.gpsimd, a, b, gates[:].rearrange("p (c s) -> p c s", s=RUN))

        codes = {}
        planes = {}

        def quantize(n):
            a, b = SPANS[n]
            codes[n] = keep.tile([P, b - a], U32, name="codes%d" % n, align_bytes=64)
            planes[n] = keep.tile([P, b - a], U8, name="plane%d" % n, align_bytes=64)
            nc.vector.quantize_mx(out=codes[n][:].bitcast(FP8X4), scales=planes[n][:], in_=rounded(a, b).rearrange("p s j -> p (s j)"))

        def multiply(target, h, first, end):
            for e in range(first, end):
                n = [n for n, (a, b) in enumerate(SPANS) if a <= e * C < b][0]
                cols = slice(e * C - SPANS[n][0], (e + 1) * C - SPANS[n][0])
                nc.tensor.matmul_mx(
                    out=target[:, (e - first) * C : (e - first + 1) * C],
                    lhsT=w_codes[:, e, 2 * P * h : 2 * P * (h + 1)].bitcast(FP4X4),
                    lhsT_scale=w_plane[:, e, P * h : P * (h + 1)],
                    rhs=codes[n][:, cols].bitcast(FP8X4),
                    rhs_scale=planes[n][:, cols],
                    start=True,
                    stop=True,
                )

        def gather(j, a, b):
            nc.scalar.activation(staged(a, b)[:, j, :], window(j, a, b), COPY)

        nc.vector.tensor_copy(staged(LAST, S)[:, 0, :], window(0, LAST, S))
        for j in range(PACK):
            if j < 3:
                gather(j, FUSED, EARLY_END)
            nc.vector.tensor_tensor(fused_stage[:, j, :], window(j, 0, FUSED), fused_gates, MULT)
        nc.vector.tensor_copy(staged(FUSED, EARLY_END)[:, 3, :], window(3, FUSED, EARLY_END))
        nc.gpsimd.tensor_scalar(rounded(0, FUSED), fused_stage[:].rearrange("p j s -> p s j"), 1.0, 0.0, MULT, ADD)
        weigh_on_gpsimd(FUSED, EARLY_POOL_END, early_gates)
        weigh(EARLY_POOL_END, EARLY_CUT, 0, EARLY_POOL_END - (EARLY_CUT - 512))
        in_runs(nc.vector, EARLY_CUT, EARLY_END, spread_gates[2][:, :P].rearrange("p (c s) -> p c s", s=RUN))
        for j in range(PACK):
            gather(j, EARLY_END, LAST)
        for j in range(1, PACK):
            gather(j, LAST, S)
        quantize(0)
        quantize(1)
        weigh_on_gpsimd(LATE_POOL, LAST, late_gates)
        weigh(EARLY_END, LATE_POOL, 1, 0)
        weigh(LAST, S, 1, LAST - EARLY_END)
        quantize(2)
        quantize(3)

        y = [keep.tile([P, S], F32, name="y0"), keep.tile([P, S], F32, name="y1", tag="y1")]

        def empty(copy, source, h, first, end):
            copy(y[h][:, first * C : end * C], source[:, : (end - first) * C])

        a, b, c, d, e = [bank(tag) for tag in "abcde"]
        g0 = bank("g0")
        multiply(g0, 0, 0, 4)
        multiply(a, 0, 4, 8)
        multiply(b, 1, 0, 4)
        multiply(c, 1, 4, 8)
        g1 = bank("g1")
        multiply(g1, 0, 8, 10)
        multiply(d, 0, 10, 12)
        g2 = bank("g2")
        multiply(g2, 1, 8, 10)
        multiply(e, 1, 10, 12)
        empty(nc.scalar.copy, g0, 0, 0, 4)
        empty(nc.scalar.copy, a, 0, 4, 8)
        empty(nc.scalar.copy, b, 1, 0, 4)
        empty(nc.vector.tensor_copy, c, 1, 4, 8)
        empty(nc.scalar.copy, g1, 0, 8, 10)
        empty(nc.vector.tensor_copy, d, 0, 10, 12)
        empty(nc.scalar.copy, g2, 1, 8, 10)
        empty(nc.vector.tensor_copy, e, 1, 10, 12)

        def picked(h, r, a, b):
            return y[h][:].indirect(back_lists[r][:, a // 16 : b // 16])

        sums = [[keep.tile([P, T], F32, name="sum%d_%d" % (h, r)) for r in range(4)] for h in range(2)]
        A, B = 384, 416
        terms = keep.tile([P, B + T], F32, name="terms")
        first = [terms[:, :T], sums[1][0][:]]
        second = [terms[:, B:], sums[1][1][:]]
        nc.vector.tensor_copy(first[0][:, :A], picked(0, 0, 0, A))
        nc.scalar.activation(first[0][:, A:], picked(0, 0, A, T), COPY)
        nc.scalar.activation(first[1], picked(1, 0, 0, T), COPY)
        for h, a, b in [(0, B, T), (0, 0, B), (1, 0, T)]:
            nc.vector.tensor_tensor(sums[h][2][:, a:b], picked(h, 2, a, b), first[h][:, a:b], ADD)
        for h, a, b, cuts in [(0, 0, T, (0, 256, T)), (1, 0, 320, (0, 320)), (1, 320, T, (320, T))]:
            nc.scalar.activation(second[h][:, a:b], picked(h, 1, a, b), COPY)
            for lo, hi in zip(cuts, cuts[1:]):
                nc.vector.tensor_tensor(sums[h][3][:, lo:hi], sums[h][2][:, lo:hi], second[h][:, lo:hi], ADD)
                nc.sync.dma_start(out[h * P : (h + 1) * P, lo:hi], sums[h][3][:, lo:hi])
